import numpy as np, ml_dtypes
CORES = [3,7,11,15,131,135,139,143]
N = 8
import mx_ref
BF = ml_dtypes.bfloat16
def gentries(a):
    return np.ascontiguousarray(a.reshape(8, 16, -1).transpose(0, 2, 1)).reshape(8, -1)
def gtable(e):
    e = np.asarray(e); return np.ascontiguousarray(e.reshape(8, -1, 16).transpose(0, 2, 1)).reshape(128, -1).astype(np.int32)
def gcols(t, e):
    v = np.concatenate([t.reshape(8, 16, -1, 4), np.zeros((8, 16, 1, 4), BF)], axis=2)
    return np.ascontiguousarray(np.stack([v[g][:, e[g]] for g in range(8)])).reshape(128, -1)
def tile(rs):
    return np.stack(rs, axis=2).reshape(128, -1).astype(BF)
def pick(q, e):
    c = np.concatenate([q[0].reshape(128, -1, 4), np.zeros((128, 1, 4), np.uint8)], axis=1); s = np.concatenate([q[1], np.ones((16, 1), np.uint8)], axis=1)
    return (np.ascontiguousarray(c[:, e].reshape(128, -1)), np.ascontiguousarray(s[:, e]))
def join(*qs):
    return (np.concatenate([q[0] for q in qs], axis=1), np.concatenate([q[1] for q in qs], axis=1))
def put(q, e, v):
    c, s = q[0].reshape(128, -1, 4).copy(), q[1].copy(); c[:, e] = v[0].reshape(128, -1, 4); s[:, e] = v[1]
    return (c.reshape(128, -1), s)
def pk(c, s):
    return (np.ascontiguousarray(c), mx_ref.live(s))
def emit(q):
    return q[0], q[1]
def packed(v, rng):
    q = [mx_ref.quantize(np.ascontiguousarray(v[r])) for r in range(N)]
    return np.stack([a for a, b in q]), np.stack([mx_ref.plane(b, rng) for a, b in q])
def values_of_codes():
    e, c = np.zeros((128, 128, 4), np.float32), np.zeros((128, 2, 4), np.uint8)
    e[np.arange(128), np.arange(128), 0] = 1
    c[:127, :, 0] = np.arange(256).reshape(2, 128).T[:127]
    return mx_ref.matmul(mx_ref.quantize(e.reshape(128, 512).astype(BF)), (c.reshape(128, 8), np.full((16, 2), 127, np.uint8))).T.reshape(-1).astype(np.float64)
CODE_VALUE, SCALE_VALUE = values_of_codes(), 2.0 ** (np.arange(256) - 127.0)
def decode(q):
    return (CODE_VALUE[q[0]].reshape(16, 8, -1, 4) * SCALE_VALUE[q[1]][:, None, :, None] + 0.0).reshape(128, -1).astype(np.float32)
def f(rng, *shape):
    return mx_ref.flush((rng.standard_normal(shape, dtype=np.float32) * np.exp2(rng.integers(-2, 3, shape[:-1] + (1,)))).astype(BF))
def wide(rng, *shape, cols=0):
    v = rng.standard_normal(shape, dtype=np.float32) * np.exp2(rng.integers(-12, 13, shape)).astype(np.float32)
    if cols: v *= np.repeat(np.exp2(rng.integers(-cols, cols + 1, shape[:-2] + (1, shape[-1] // 4))) * (rng.random(shape[:-2] + (1, shape[-1] // 4)) > 0.0625), 4, axis=-1).astype(np.float32)
    return mx_ref.flush(v.astype(BF))
C, HALF, E = 288, 144, 224
MASK = [4, 1, 2]
TIMES = 9
def register(b):
    a = 2 * np.arange(HALF)
    return np.concatenate([a + b, a + 1 - b], axis=-1)
def lowest(s):
    low, to = np.broadcast_to(np.arange(C), s.shape), s
    for i in range(TIMES):
        low = np.minimum(low, np.take_along_axis(low, to, axis=-1))
        to = np.take_along_axis(to, to, axis=-1)
    return low
def joined(s):
    low, c = lowest(s), np.arange(HALF)
    a, b = low[..., :HALF], low[..., HALF:]
    swap = (a != b) & ((a == c) & (c > 0) | (b == c + HALF))
    return np.concatenate([np.where(swap, s[..., HALF:], s[..., :HALF]), np.where(swap, s[..., :HALF], s[..., HALF:])], axis=-1)
def numbers_of(rng):
    return {"x": np.array(f(rng, N, 128, 4 * C)), "u": np.array(f(rng, N, 128, 512)), "v": np.array(f(rng, N, 128, 512))}
def orders(rng):
    return rng.permuted(np.tile(np.arange(C), (N, 8, 1)), axis=2)
def stored(k):
    return {"kl": np.stack([gtable(k[r]) for r in range(N)])}
def layers(rng):
    return np.array(f(rng, N, 128, 2048)).reshape(N, 8, 16, 4, 8, 16, 4)
def weights(rng, w):
    c, p = packed(np.ascontiguousarray(w).reshape(N, 128, 2048), rng)
    return {"wc": c, "ws": p}
def setup_inputs(rng):
    return {**numbers_of(rng), **stored(orders(rng)), **weights(rng, layers(rng))}
def setup_inputs_ties(rng):
    d = numbers_of(rng)
    o = rng.permutation(N)
    k = rng.integers(-1, 2, (N, 8, C)).astype(np.float32)
    k[o[1]] = 1
    x = d["x"].reshape(N, 8, 16, C, 4)
    x[:, :, 0] = 0
    x[:, :, 0, :, 0] = k.astype(BF)
    a = np.exp2(rng.integers(-3, 4, (8, 1)).astype(np.float64))
    j = rng.integers(3, 7, (8, 4, 6))
    j[:, :, 0] = 6
    q = (9 + 2 * rng.integers(0, 4, (8, 4, 6))) * 0.125 * np.exp2(-j.astype(np.float64))
    x[:, :, 8:] = 0
    x[:, :, 8, :, 0] = (-3.0 * a).astype(np.float32).astype(BF)
    x[:, :, 10, :, 0] = (-0.140625 * a).astype(np.float32).astype(BF)
    x[:, :, 10, :, 1] = (-0.125 * a).astype(np.float32).astype(BF)
    c = np.ones(N, np.float32)
    c[o[0]] = 0
    c[o[2]] = -1
    u = d["u"].reshape(N, 128, 128, 4)
    u[:, :, ::16] = 0
    for h in range(0, 128, 16): u[:, h, h, 0] = c.astype(BF)
    w = layers(rng)
    w[:, :, 0] = 0
    w[:, :, :, :, :, 0] = 0
    w[:, :, :, :, :, 8:] = 0
    for g in range(8): w[:, g, 10, 0, g, 8, 0] = -224.0
    for n, i in enumerate((9, 11, 12, 13, 14, 15)):
        x[:, :, i] = (q[:, :, n] * a * -0.0078125)[:, None].astype(np.float32).astype(BF)
        for g in range(8): w[:, g, 10, :, g, i, 1] = (-q[g, :, n]).astype(np.float32).astype(BF)
    return {"x": x.reshape(N, 128, 4 * C), "u": u.reshape(N, 128, 512), "v": d["v"], **stored(orders(rng)), **weights(rng, w)}
def setup_inputs_near(rng):
    d = numbers_of(rng)
    o = rng.permutation(N) % 4
    k = np.where((o == 1) | (o == 2), 1.0, 2.0 ** -30).astype(np.float32)
    x = d["x"].astype(np.float32).reshape(N, 8, 16, C, 4)
    x[:, :, :8] = 0
    s = rng.integers(-1, 2, (N, 8, C)) * k[:, None, None]
    s[o == 3] = 0
    x[:, :, 0, :, 0] = 1.125 * s
    x[:, :, 1, :, 0] = -1.25 * s
    x[:, :, 7, :, 0] = 2.0 ** -30
    w = layers(rng)
    w[:, :, :8] = 0
    w[:, :, :, :, :, :8] = 0
    for r in range(N):
        if o[r] == 3:
            x[r, :, 4, :, 0] = rng.choice([-1.0, 1.0], (8, C)) * 2.0 ** -30
            for g in range(8):
                w[r, g, 4, 0, g, 0, 0] = 1.125 * 2.0 ** -8
                w[r, g, 4, 0, g, 1, 0] = -1.25 * 2.0 ** -8
                w[r, g, 7, 0, g, 6, 0] = 2.0 ** 5
        at = [0, C - 1, int(rng.integers(C)), int(rng.integers(C))]
        for g, j in zip(rng.permutation(8)[:4], at): x[r, g, 0, j, 0] = 2.0 ** 30 * rng.choice([-1.0, 1.0])
    u = d["u"].reshape(N, 128, 128, 4)
    u[:, :, ::16] = 0
    for h in range(0, 128, 16):
        u[:, h, h, 0] = (1.125 * k).astype(np.float32).astype(BF)
        u[:, h + 1, h, 0] = k.astype(BF)
    return {"x": x.reshape(N, 128, 4 * C).astype(BF), "u": u.reshape(N, 128, 512), "v": d["v"], **stored(orders(rng)), **weights(rng, w)}
def setup_inputs_long(rng):
    d = numbers_of(rng)
    k = orders(rng)
    b = rng.integers(0, 2, (N, 8, HALF))
    for c in rng.permutation(HALF):
        low = lowest(register(b))
        b[..., c] ^= (low[..., c] != low[..., c + HALF]).astype(np.int64)
    last = HALF - 1 - (HALF - 1) // 2
    way = [last >> i for i in range(last.bit_length() - 1, -1, -1)]
    for r in range(N):
        t = rng.permutation(8)
        for g in t[2:4]: b[r, g, rng.integers(1, HALF)] ^= 1
        b[r, t[4], 0] ^= 1
        for g in t[5:]: b[r, g] = rng.integers(0, 2, HALF)
        for g in t[5:7]:
            b[r, g, HALF - 1] = 0
            for i, j in zip(way, way[1:]): b[r, g, HALF - 1 - i] = j & 1
            b[r, g, HALF - 1 - last] = 1 - (HALF - 1) % 2
    s = np.zeros((N, 8, C))
    np.put_along_axis(s, k, np.concatenate([b, rng.integers(0, 2, (N, 8, HALF))], axis=2) * 2.0 - 1.0, axis=2)
    x = d["x"].reshape(N, 8, 16, C, 4)
    x[:, :, 0] = 0
    x[:, :, 0, :, 0] = (s * np.exp2(rng.integers(-3, 4, (N, 8, C)).astype(np.float64))).astype(np.float32).astype(BF)
    u = d["u"].reshape(N, 128, 128, 4)
    u[:, :, ::16] = 0
    for h in range(0, 128, 16): u[:, h, h, 0] = 1
    w = layers(rng)
    w[:, :, :, :, :, 0] = (w[:, :, :, :, :, 0].astype(np.float32) * 4).astype(BF)
    return {"x": x.reshape(N, 128, 4 * C), "u": u.reshape(N, 128, 512), "v": d["v"], **stored(k), **weights(rng, w)}
def setup_inputs_ends(rng):
    d = numbers_of(rng)
    o, e = rng.permutation(N) % 4, rng.permutation(N) % 4
    k = orders(rng)
    x = np.zeros((N, 8, 16, C, 4))
    u = d["u"].astype(np.float32).reshape(N, 128, 128, 4)
    v = np.zeros((N, 128, 512))
    w = np.zeros((N, 128, 4, 128, 4), np.float32)
    i = np.arange(128)[np.arange(128) % 16 < 15]
    j = np.arange(14, 128, 16)
    up, down = np.arange(C), np.arange(C)[::-1]
    for r in range(N):
        if e[r] == 0: k[r] = up
        if e[r] == 1: k[r] = down
        if e[r] == 2: k[r] = np.where(rng.permutation(8)[:, None] < 4, up, down)
        h = rng.permutation(8)
        c = np.where(h < 2, 0.0, h % 2 * 2.0 - 1.0)[None, :, None]
        much = (0.9 + 0.1 * rng.random((8, 16, C, 4))) * 2.0 ** 29
        if o[r] == 0: x[r] = -much
        if o[r] == 1: x[r] = much * rng.choice([-1.0, 1.0], (1, 1, C, 1))
        if o[r] == 2: x[r] = -(1.0 + 0.125 * rng.integers(0, 8, (8, 16, C, 4))) * 2.0 ** -30
        if o[r] == 3: x[r] = d["x"][r].astype(np.float32).reshape(8, 16, C, 4)[:, :, :1]
        x[r, :, 15] = 2.0 ** -30
        if o[r] < 2:
            u[r, :, ::16] = c * (0.9 + 0.1 * rng.random((128, 8, 4))) * 2.0 ** 30
            v[r] = (0.9 + 0.1 * rng.random((128, 512))) * 2.0 ** 30
        else:
            v[r] = (1.0 + 0.125 * rng.integers(0, 8, (128, 512))) * 2.0 ** -30
        if o[r] == 2: u[r, :, ::16] = c * (1.0 + 0.125 * rng.integers(0, 8, (128, 8, 4))) * 2.0 ** -30
        if o[r] == 3: u[r, :, ::16] *= np.abs(c).astype(np.float32)
        n = np.array([1.0, 2.0, 4.0])[rng.permutation(8) % 3]
        for b in range(4):
            if o[r] != 2: w[r, i, b, i, b] = -n[i // 16]
            else:
                w[r, i, b, i, b] = -2.0 ** -8
                w[r, j, b, j, b] = 0.0
                w[r, j + 1, b, j, b] = 2.0 ** 8
                w[r, j - 8, b, j - 8, b] = 0.0
                w[r, j + 1, b, j - 8, b] = 2.0 ** 5
    v = v * rng.choice([-1.0, 1.0], (N, 128, 512))
    return {"x": x.astype(np.float32).reshape(N, 128, 4 * C).astype(BF), "u": u.reshape(N, 128, 512).astype(BF), "v": v.astype(np.float32).astype(BF), **stored(k), **weights(rng, w.astype(BF))}
def setup_inputs_spread(rng):
    d = setup_inputs(rng)
    d["x"] = wide(rng, N, 128, 4 * C, cols=6)
    return d
def check_inputs(d):
    b = []
    for k in ("x", "u", "v"):
        a = np.abs(d[k].astype(np.float32))
        if not (np.isfinite(a).all() and ((a == 0) | (a >= 2.0 ** -30) & (a <= 2.0 ** 30)).all()): b.append("a value of " + k)
    none, least, most = [emit(mx_ref.quantize(np.full((128, 16), k, np.float32).astype(BF)))[1][0, 0] for k in (0.0, 2.0 ** -8, 2.0 ** 8)]
    for r in range(N):
        if not (np.sort(gentries(d["kl"][r]), axis=1) == np.arange(C)).all(): b.append("kl: not a permutation")
        if ((d["wc"][r] == 0x7F) | (d["wc"][r] == 0xFF)).any(): b.append("wc: a code that is no number")
        s = mx_ref.live(d["ws"][r])
        if ((s != none) & ((s < least) | (s > most))).any(): b.append("ws: a scale out of range")
    return b
def reference(x, u, v, kl, wc, ws):
    qu = [mx_ref.quantize(u[r]) for r in range(N)]
    lay = [pk(wc[r], ws[r]) for r in range(N)]
    now = [x[r] for r in range(N)]
    k = [gentries(kl[r]).astype(np.int64) for r in range(N)]
    for m in MASK:
        e, made = [], []
        for r in range(N):
            s = mx_ref.matmul(qu[r], mx_ref.quantize(now[r]))[::16]
            bits = (np.take_along_axis(s, k[r][:, :HALF], axis=1) > 0).astype(np.int64)
            e.append(np.take_along_axis(k[r], joined(register(bits)), axis=1))
            z = (gcols(now[r], k[r]).astype(np.float32) + gcols(now[r], e[r]).astype(np.float32)) * np.float32(0.5)
            q = mx_ref.quantize(z.astype(BF))
            made.append(tile([mx_ref.matmul(pick(lay[r], np.arange(128 * b, 128 * b + 128)), q) * np.float32(0.03125) for b in range(4)]))
        k = [np.take_along_axis(k[r ^ m], e[r], axis=1) for r in range(N)]
        for r in range(N):
            far = decode(mx_ref.quantize(np.ascontiguousarray(made[r ^ m][:, :4 * E]))).astype(BF)
            both = np.concatenate([far, made[r][:, 4 * E:]], axis=1)
            now[r] = (now[r].astype(np.float32) + gcols(both, k[r]).astype(np.float32)).astype(BF)
    y, kp = np.zeros((N, 128, C), np.float32), np.zeros((N, 8, C), np.float32)
    oc, osc = np.zeros((N, 128, 4 * C), np.uint8), np.zeros((N, 16, C), np.uint8)
    for r in range(N):
        q = mx_ref.quantize(now[r])
        y[r] = mx_ref.matmul(mx_ref.quantize(v[r]), q)
        kp[r] = k[r]
        oc[r], osc[r] = emit(q)
    return {"y": y, "kp": kp, "oc": oc, "osc": osc}

@@ -1,0 +1,565 @@
+from concourse.bass import DstId, RemoteDMATransfer
+from concourse.mybir import dt, AluOpType, AxisListType, ActivationFunctionType
+
+C, HALF, E = 288, 144, 224
+MASKS = [4, 1, 2]
+HS = ((0, 160), (160, 288))
+C1 = 128
+C2 = E - C1
+F4 = "float8_e4m3fn_x4"
+
+SCRATCH = {
+    "ub": ("sbuf", [128, 512], "bfloat16"), "vb": ("sbuf", [128, 512], "bfloat16"), "et": ("sbuf", [128, 2048], "bfloat16"),
+    "one": ("sbuf", [128, 512], "bfloat16"),
+    "uq": ("sbuf", [128, 128], F4), "us": ("sbuf", [128, 128], "uint8"),
+    "ur": ("sbuf", [128, 128], F4), "urs": ("sbuf", [128, 128], "uint8"),
+    "vq": ("sbuf", [128, 128], F4), "vs": ("sbuf", [128, 128], "uint8"),
+    "eq": ("sbuf", [128, 512], F4), "es": ("sbuf", [128, 512], "uint8"),
+    "wq": ("sbuf", [128, 512], F4), "wp": ("sbuf", [128, 512], "uint8"),
+    "kli": ("sbuf", [128, 18], "int32"), "ki": ("sbuf", [128, 54], "int32"),
+    "kld": ("dram", [128, 18], "int32"), "lk0": ("dram", [128, 18], "int32"),
+    "nd1": ("dram", [128, 18], "float32"), "nd2": ("dram", [128, 18], "float32"),
+    "lk1": ("dram", [128, 18], "float32"), "lk2": ("dram", [128, 18], "float32"),
+    "kf0": ("sbuf", [128, C], "int32"), "kf1": ("sbuf", [128, C], "float32"), "kf2": ("sbuf", [128, C], "float32"),
+    "pI": ("sbuf", [128, 8], "int32"), "uI": ("sbuf", [128, 8], "int32"), "pF": ("sbuf", [128, 24], "float32"),
+    "uo": ("sbuf", [128, 8], "uint16"),
+    "ks": ("sbuf", [128, 18], "uint16"),
+    "oAD": ("sbuf", [128, 10], "uint16"), "oBC": ("sbuf", [128, 10], "uint16"), "oRi": ("sbuf", [128, 6], "uint16"),
+    "o4": ("sbuf", [128, 4], "uint16"), "oVC": ("sbuf", [128, 6], "uint16"), "oR": ("sbuf", [128, 6], "uint16"),
+    "tt4": ("sbuf", [128, 72], "uint16"), "tt18": ("sbuf", [128, 18], "uint16"),
+    "ps": ("psum", [128, 4096], "float32"),
+    "ysb": ("sbuf", [128, C], "float32"),
+}
+for _i in range(4):
+    SCRATCH["X%d" % _i] = ("sbuf", [128, 4 * C], "bfloat16")
+    SCRATCH["xq%d" % _i] = ("sbuf", [128, C], F4)
+    SCRATCH["xs%d" % _i] = ("sbuf", [128, C], "uint8")
+    SCRATCH["oP%d" % _i] = ("sbuf", [128, 6], "uint16")
+    SCRATCH["kt%d" % _i] = ("sbuf", [128, 18], "uint16")
+for _i in range(3):
+    SCRATCH["XK%d" % _i] = ("sbuf", [128, 4 * C], "bfloat16")
+    SCRATCH["XC%d" % _i] = ("sbuf", [128, 4 * C], "bfloat16")
+    SCRATCH["Z%d" % _i] = ("sbuf", [128, 4 * C], "bfloat16")
+    SCRATCH["H%d" % _i] = ("sbuf", [128, 4 * E], "bfloat16")
+    SCRATCH["B%d" % _i] = ("sbuf", [128, 4 * C], "bfloat16")
+    SCRATCH["zq%d" % _i] = ("sbuf", [128, C1 + 256], F4)
+    SCRATCH["zs%d" % _i] = ("sbuf", [128, C1 + 256], "uint8")
+    SCRATCH["hq%d" % _i] = ("sbuf", [128, C1 + 128], F4)
+    SCRATCH["hs%d" % _i] = ("sbuf", [128, C1 + 128], "uint8")
+    SCRATCH["lq%d" % _i] = ("sbuf", [128, E], F4)
+    SCRATCH["ls%d" % _i] = ("sbuf", [128, E], "uint8")
+    SCRATCH["k4t%d" % _i] = ("sbuf", [128, 80], "uint16")
+    SCRATCH["nf%d" % _i] = ("sbuf", [128, C], "float32")
+    SCRATCH["kk%d" % _i] = ("sbuf", [128, C], "float32")
+_ROWS = {
+    "t16": 288, "t4": 288, "t8": 80, "t2": 80, "t32": 288, "J1": 80, "J2": 80, "q16": 16, "q32": 40, "m144": 288, "tmp": 288,
+    "W1": 288, "W2": 288, "W3": 288, "W4": 288, "W5": 288, "cAD": 144, "sgM": 144, "M16n": 288, "M4n": 288, "M2": 80, "M8": 80,
+    "m8z": 80, "d16": 80, "JM2": 80, "JM8": 80,
+    "cT": 16, "tA": 16, "tB": 16, "tC": 16, "tD": 16, "tcAD": 16, "tcBC": 16, "sgT": 16, "tb": 16, "cc18": 16,
+    "b1": 40, "cc4": 40, "bits": 288, "fl": 144, "BC": 16, "tw": 32, "ts": 32,
+    "Vw": 80, "Vs": 80, "Vb": 80, "F0": 80, "F1": 80, "F2": 80, "G0": 80, "G1": 80, "G2": 80,
+    "l0": 80, "l1": 80, "l2": 80, "l3": 80, "l4": 80, "l5": 80, "l6": 80, "l7": 80, "lc": 80,
+    "fM2": 80, "dj": 40, "s1": 40, "fs": 40, "x4": 240, "z4": 216, "xs4": 216, "tab2": 40,
+    "fM8": 80, "fS8": 80, "f18": 16, "s18": 16, "fs18": 16, "x8": 240, "z8": 216, "xs8": 216, "up": 16,
+}
+_ROWS2 = {
+    "x2": 288, "z2": 288, "xs2": 288, "n4w": 288, "n4s": 288, "n16w": 288, "n16s": 288, "d4": 288, "d16b": 288,
+    "Pw": 80, "Ps": 80, "Rw": 80, "Rs": 80, "Gw": 80, "Gs": 80, "fM4": 144, "fS4": 144, "m4z": 144,
+}
+OFF = {}
+for _b, _t, _d in (("F", _ROWS, "float32"), ("G", _ROWS2, "bfloat16")):
+    _n = 0
+    for _k, _v in _t.items():
+        OFF[_k] = (_b, _n, _v)
+        _n += (_v + 15) // 16 * 16
+    SCRATCH[_b] = ("sbuf", [128, _n], _d)
+
+SEMAPHORES = ["v", "s", "p", "q", "sent", "dx0", "dx1", "dk", "du", "dw", "dv", "dkl", "dn1", "dn2", "df0", "df1", "df2", "dout",
+              "lr0", "lr1", "lr2", "ha0", "ha1", "ha2", "hb0", "hb1", "hb2"]
+
+
+def rank_program(g, core, T, topo):
+    rank = T.rank_of(core)
+    if rank is None:
+        return
+    A = AluOpType
+    COPY, IDENT, SIGN = ActivationFunctionType.Copy, ActivationFunctionType.Identity, ActivationFunctionType.Sign
+    queue = {"v": g.vector, "s": g.scalar, "p": g.tensor, "q": g, "y": g.sync}
+    total, known, log = {}, {}, {}
+
+    def f(name, a=0, b=None, step=1):
+        o = OFF[name]
+        return (o[0], o[1] + a, o[1] + (o[2] if b is None else b), step)
+
+    def t(name, a=0, b=None, step=1):
+        return (name, a, SCRATCH[name][1][1] if b is None else b, step)
+
+    def ap(x):
+        return T[x[0]][:, x[1]:x[2]:x[3]] if x[3] != 1 else T[x[0]][:, x[1]:x[2]]
+
+    def ind(win, off):
+        return ap(win).indirect(ap(off))
+
+    def clash(x, y):
+        if x[0] != y[0] or x[1] >= y[2] or y[1] >= x[2]:
+            return False
+        if x[3] == y[3] and x[3] > 1 and (x[1] - y[1]) % x[3]:
+            return False
+        return True
+
+    def need(q, sem, val):
+        if known.get((q, sem), 0) < val:
+            queue[q].wait_ge(T.sem[sem], val)
+            known[(q, sem)] = val
+
+    def order(q, reads, writes):
+        want = {}
+        for rw, views in ((0, reads), (1, writes)):
+            for x in views:
+                for y, w, sem, val in log.get(x[0], ()):
+                    if (rw or w) and clash(x, y):
+                        want[sem] = max(want.get(sem, 0), val if val else total[sem])
+        for sem in want:
+            need(q, sem, want[sem])
+
+    def note(sem, val, reads, writes):
+        for x in writes:
+            log[x[0]] = [e for e in log.get(x[0], []) if not (e[0][1] >= x[1] and e[0][2] <= x[2] and (x[3] == 1 or x == e[0]))]
+            log[x[0]].append((x, 1, sem, val))
+        for x in reads:
+            log.setdefault(x[0], []).append((x, 0, sem, val))
+
+    def run(q, call, reads, writes):
+        psum = [("ps", x[1] // 512 * 512, x[1] // 512 * 512 + 512, 1) for x in reads + writes if x[0] == "ps"]
+        reads, writes = [x for x in reads if x[0] != "ps"], [x for x in writes if x[0] != "ps"] + psum
+        order(q, reads, writes)
+        total[q] = total.get(q, 0) + 1
+        call().then_inc(T.sem[q], 1)
+        note(q, total[q], reads, writes)
+
+    def dma(q, sem, out, in_, reads, writes):
+        order(q, reads, writes)
+        total[sem] = total.get(sem, 0) + 16
+        queue[q].dma_start(out, in_).then_inc(T.sem[sem], 16)
+        note(sem, 0, reads, writes)
+
+    def tt(out, a, b, op):
+        run("v", lambda: g.vector.tensor_tensor(ap(out), ap(a), ap(b), op), [a, b], [out])
+
+    def ts(out, a, s1, op0, s2=None, op1=None):
+        sc = [x for x in (s1, s2) if isinstance(x, tuple)]
+        u1 = ap(s1) if isinstance(s1, tuple) else s1
+        u2 = ap(s2) if isinstance(s2, tuple) else s2
+        if op1 is None:
+            run("v", lambda: g.vector.tensor_scalar(ap(out), ap(a), u1, None, op0), [a] + sc, [out])
+        else:
+            run("v", lambda: g.vector.tensor_scalar(ap(out), ap(a), u1, u2, op0, op1), [a] + sc, [out])
+
+    def cp(out, a):
+        run("v", lambda: g.vector.tensor_copy(ap(out), ap(a)), [a], [out])
+
+    def gat(out, win, off):
+        run("v", lambda: g.vector.tensor_copy(ap(out), ind(win, off)), [win, off], [out])
+
+    def gop(out, win, off, b, op):
+        run("v", lambda: g.vector.tensor_tensor(ap(out), ind(win, off), ap(b), op), [win, off, b], [out])
+
+    def scan(out, d0, d1, op0, op1):
+        run("v", lambda: g.vector.tensor_tensor_scan(ap(out), ap(d0), ap(d1), 0.0, op0, op1), [d0, d1], [out])
+
+    def act(out, a, scale=1.0):
+        run("s", lambda: g.scalar.activation(ap(out), ap(a), COPY, scale=scale), [a], [out])
+
+    def acts(out, a, col):
+        run("s", lambda: g.scalar.activation(ap(out), ap(a), COPY, scale=ap(col)), [a, col], [out])
+
+    def actf(out, a, func, scale, bias):
+        if isinstance(bias, tuple):
+            run("s", lambda: g.scalar.activation(ap(out), ap(a), func, bias=ap(bias), scale=scale), [a, bias], [out])
+        else:
+            run("s", lambda: g.scalar.activation(ap(out), ap(a), func, bias=bias, scale=scale), [a], [out])
+
+    def equal(out, a, col, tmp):
+        actf(tmp, a, ActivationFunctionType.Abs, -1.0, col)
+        actf(out, tmp, ActivationFunctionType.Relu, -1.0, 1.0)
+
+    def actg(out, win, off, scale=1.0, bias=None):
+        if bias is None:
+            run("s", lambda: g.scalar.activation(ap(out), ind(win, off), COPY, scale=scale), [win, off], [out])
+        else:
+            run("s", lambda: g.scalar.activation(ap(out), ind(win, off), IDENT, bias=bias), [win, off], [out])
+
+    def fill(out, c):
+        run("v", lambda: g.vector.memset(ap(out), c), [], [out])
+
+    def quant(q, s, a):
+        run("v", lambda: g.vector.quantize_mx(ap(q), ap(s), ap(a)), [a], [q, s])
+
+    def mm(out, l, ls, r, rs):
+        run("p", lambda: g.tensor.matmul_mx(ap(out), ap(l), ap(ls), ap(r), ap(rs), True, True), [l, ls, r, rs], [out])
+
+    def iota(out, pattern, base=0, cm=0):
+        if out[0] == "F":
+            run("q", lambda: g.iota(ap(out), pattern, base, cm, allow_small_or_imprecise_dtypes=True), [], [out])
+        else:
+            run("q", lambda: g.iota(ap(out), pattern, base, cm), [], [out])
+
+    def bank(i, n):
+        i %= 8
+        return ("ps", 512 * i, 512 * i + n, 1)
+
+    def send(dst, sem, out, in_, reads, bits=False):
+        order("q", reads, [])
+        rid, pid = topo.addr(dst, core)
+        n = len(topo.engines(core, dst))
+        o, i = (ap(out).bitcast(dt.uint8), ap(in_).bitcast(dt.uint8)) if bits else (ap(out), ap(in_))
+        if SCRATCH[out[0]][0] == "dram":
+            o, i = T[out[0]][:, :], T[in_[0]][:, :]
+        total["sent"] = total.get("sent", 0) + n
+        g.remote_dma(o, i, T.sem[sem], T.sem.sent, pid, rid, topo.mask(core, dst))
+        return n
+
+    def arrives(sem, n, writes):
+        total[sem] = total.get(sem, 0) + n
+        note(sem, 0, [], writes)
+
+    dma("y", "dx0", T.X0[:, 0:640], T.x[:, 0:640], [], [t("X0", 0, 640)])
+    dma("s", "dk", T.kli[:, :], T.kl[:, :], [], [t("kli")])
+    dma("s", "du", T.ub[:, :], T.u[:, :], [], [t("ub")])
+    dma("y", "dx1", T.X0[:, 640:1152], T.x[:, 640:1152], [], [t("X0", 640, 1152)])
+    dma("y", "dkl", T.kld[:, :], T.kl[:, :], [], [t("kld")])
+    need("y", "dx1", 16)
+    dma("y", "dw", T.wq[:, 0:512].bitcast(dt.uint8), T.wc[:, :], [], [t("wq")])
+    dma("y", "dw", T.wp[:, 0:512], T.ws[:, :], [], [t("wp")])
+    dma("y", "dv", T.vb[:, :], T.v[:, :], [], [t("vb")])
+
+    iota(t("pI", 0, 1), [[0, 1]], 0, 1)
+    iota(t("uI"), [[16, 8]])
+    iota(f("t16"), [[0, 18], [1, 16]])
+    iota(f("q16", 0, 9), [[16, 9]])
+    iota(f("t32"), [[0, 9], [1, 32]])
+    iota(f("t2"), [[0, 40], [1, 2]])
+    iota(f("t8"), [[0, 10], [1, 8]])
+    iota(f("J1"), [[1, 80]], 1)
+    iota(f("q32", 0, 36), [[32, 36]])
+    for i, base in enumerate((72, 216, 1, 145)):
+        iota(f("cAD", 36 * i, 36 * i + 36), [[2, 36]], base)
+    iota(f("W1"), [[1, 288]])
+    iota(f("t4"), [[0, 72], [1, 4]])
+    partner = [T.cores[rank ^ m] for m in MASKS]
+    arrives("lr0", send(partner[0], "lr0", t("lk0"), t("kld"), [t("kld")]), [t("lk0")])
+
+    def pcol(i):
+        return t("pF", i, i + 1)
+
+    cp(t("uo"), t("uI"))
+    ts(t("pI", 1, 2), t("pI", 0, 1), 15, A.bitwise_and)
+    ts(t("pI", 2, 3), t("pI", 0, 1), 3, A.bitwise_and)
+    ts(t("pI", 3, 4), t("pI", 0, 1), 15, A.bitwise_and, 2, A.arith_shift_right)
+    ts(t("pI", 4, 5), t("pI", 0, 1), 15, A.bitwise_and, 3, A.arith_shift_right)
+    ts(t("pI", 5, 6), t("pI", 0, 1), 15, A.bitwise_and, 1, A.arith_shift_right)
+    ts(t("pI", 6, 7), t("pI", 0, 1), 2, A.arith_shift_right, 1, A.bitwise_and)
+    ts(t("pI", 7, 8), t("pI", 0, 1), 1, A.bitwise_and)
+    cp(t("pF", 0, 8), t("pI"))
+    P16, P4, I4, I8, I2, PAR4, PAR2 = [pcol(i) for i in range(1, 8)]
+    equal(f("M16n"), f("t16"), P16, f("tmp"))
+    act(f("sgM", 0, 72), f("M16n", 0, 72))
+    act(f("sgM", 72, 144), f("M16n", 72, 144), -1.0)
+    actf(f("z2"), f("t32"), SIGN, 1.0, 0.0)
+    actf(f("d16"), f("t16", 0, 80), SIGN, 1.0, 0.0)
+    fill(f("x2"), 0.0)
+    ts(f("cT", 0, 9), f("q16", 0, 9), P16, A.add)
+    ts(f("tA", 0, 9), f("cT", 0, 9), 36.0, A.is_ge, 72.0, A.mult)
+    ts(f("tB", 0, 9), f("cT", 0, 9), 108.0, A.is_ge, 72.0, A.mult)
+    ts(f("tC", 0, 9), f("cT", 0, 9), 72.0, A.is_ge, 287.0, A.mult)
+    ts(f("tD", 0, 9), f("cT", 0, 9), 2.0, A.mult, 72.0, A.add)
+    tt(f("tA", 0, 9), f("tA", 0, 9), f("tB", 0, 9), A.add)
+    tt(f("tD", 0, 9), f("tD", 0, 9), f("tC", 0, 9), A.subtract)
+    ts(f("sgT", 0, 9), f("cT", 0, 9), 72.0, A.is_ge, -2.0, A.mult)
+    ts(f("sgT", 0, 9), f("sgT", 0, 9), 1.0, A.add)
+    tt(f("tcAD", 0, 9), f("tA", 0, 9), f("tD", 0, 9), A.add)
+    tt(f("tcBC", 0, 9), f("tcAD", 0, 9), f("sgT", 0, 9), A.add)
+    ts(f("x2", 31, 288, 32), f("tcAD", 0, 9), -144.0, A.add)
+
+    def state(r, h):
+        a, b = HS[h]
+        quant(t("xq%d" % r, a, b), t("xs%d" % r, a, b), t("X%d" % r, 4 * a, 4 * b))
+
+    def scores(r, h):
+        a, b = HS[h]
+        mm(bank(2 + h, b - a), t("ur"), t("urs"), t("xq%d" % r, a, b), t("xs%d" % r, a, b))
+
+    fill(f("x4"), 0.0)
+    fill(f("z4"), -1.0)
+    fill(f("x8"), 0.0)
+    fill(f("z8"), -1.0)
+    quant(t("uq"), t("us"), t("ub"))
+    state(0, 0)
+    state(0, 1)
+    run("v", lambda: g.vector.tensor_copy(T.ur[:, 0:128].bitcast(dt.uint32), T.uq[:, 0:128].bitcast(dt.uint32).indirect(T.uo[:, 0:8])),
+        [t("uq"), t("uo")], [t("ur")])
+    run("s", lambda: g.scalar.activation(T.urs[:, 0:128], T.us[:, 0:128].indirect(T.uo[:, 0:8]), COPY), [t("us"), t("uo")], [t("urs")])
+
+    def ends(n):
+        act(f(n, 0, 72), f("W1", 0, 72))
+        act(f(n, 216, 288), f("W1", 216, 288))
+
+    actf(f("d16"), f("d16"), IDENT, 16384.0, -8192.0)
+    actf(f("M16n"), f("M16n"), IDENT, 4096.0, -4096.0)
+    ends("W2")
+    act(f("d16b", 0, 80), f("d16"))
+    ends("W3")
+    act(f("J2"), f("J1"))
+
+    scores(0, 0)
+    scores(0, 1)
+    cp(t("kt0"), t("kli"))
+    for e in range(4):
+        ts(t("k4t0", 20 * e, 20 * e + 18), t("kli"), 4, A.mult, e, A.add)
+    run("v", lambda: g.vector.memset(T.one[:, 0:512], 1.0), [], [t("one")])
+    for e in range(4):
+        run("q", lambda: g.affine_select(T.et[:, 512 * e:512 * e + 512], T.one[:, 0:512], [[-1, 512]], A.is_equal, 0.0, e, 4),
+            [t("one")], [t("et", 512 * e, 512 * e + 512)])
+
+    def constants2():
+        ts(t("pF", 16, 20), f("t4", 0, 4), I4, A.is_equal, 4.0, A.mult)
+        ts(t("pF", 20, 22), f("t4", 0, 2), I8, A.is_equal)
+        ts(t("pF", 9, 11), t("pF", 6, 8), -2.0, A.mult, 1.0, A.add)
+        ts(pcol(13), I4, 0.0, A.is_equal)
+        ts(pcol(8), I4, 8.0, A.mult, P4, A.add)
+        ts(pcol(12), P16, 15.0, A.is_equal)
+        tt(f("JM2"), f("J1"), f("M2"), A.mult)
+        tt(f("JM2", 0, 1), f("JM2", 0, 1), pcol(13), A.subtract)
+        actf(f("b1", 0, 36), f("q32", 0, 36), IDENT, 1.0, pcol(8))
+        actf(f("cc4", 0, 36), f("b1", 0, 36), IDENT, 2.0, 4.0)
+
+    def constants3():
+        ts(pcol(14), P16, 0.0, A.is_equal)
+        tt(f("JM8"), f("J1"), f("M8"), A.mult)
+        tt(f("JM8", 0, 1), f("JM8", 0, 1), pcol(14), A.subtract)
+
+    def constants4():
+        ts(f("tmp"), f("t16"), 0.0, A.is_gt, 16384.0, A.mult)
+        ts(f("d16b"), f("tmp"), -8192.0, A.add)
+
+    def table(out, src, n, step=16):
+        cp(out, (src[0], src[1] + step - 1, src[1] + n, step))
+
+    for r in range(3):
+        X, XK, XC, Z, H, B, kt = ["%s%d" % (n, r) for n in ("X", "XK", "XC", "Z", "H", "B", "kt")]
+        zq, zs, hq, hs, lq, ls, nf, kk = ["%s%d" % (n, r) for n in ("zq", "zs", "hq", "hs", "lq", "ls", "nf", "kk")]
+        kf, lk = "kf%d" % r, "lk%d" % r
+        for i in range(16):
+            dma("y", "df%d" % r, T[kf][i:128:16, :], T[lk][:, :], [t(lk)], [(kf, i, C, 16)])
+        for h in range(2):
+            ts(f("bits", HS[h][0], HS[h][1]), bank(2 + h, HS[h][1] - HS[h][0]), 0.0, A.is_gt)
+        actg(f("fl"), f("bits"), t(kt, 0, 9))
+
+        def half_of_xk(h):
+            for e in (2 * h, 2 * h + 1):
+                actg(t(XK, e, 1152, 4), t(X), t("k4t%d" % r, 20 * e, 20 * e + 18), 0.5)
+
+        half_of_xk(0)
+        if r == 0:
+            ends("W4")
+            ends("W5")
+            for m, c, i, o in (("M2", "t2", I8, 0), ("M8", "t8", I2, 80)):
+                equal(f(m), f(c), i, f("tmp", o, o + 80))
+            actf(f("m4z"), f("t4", 0, 144), SIGN, 1.0, 0.0)
+        gop(f("x2", 0, 288, 2), f("bits"), t(kt, 0, 9), f("sgM"), A.mult)
+        scan(f("xs2"), f("z2"), f("x2"), A.mult, A.add)
+        sd = f("xs2", 30, 288, 32)
+        ts(t("oAD", 0, 9), f("xs2", 31, 288, 32), 144.0, A.add)
+        tt(f("BC", 0, 9), f("tcBC", 0, 9), sd, A.subtract)
+        tt(f("W1", 72, 144), f("cAD", 0, 72), f("fl", 0, 72), A.add)
+        tt(f("W1", 144, 216), f("cAD", 72, 144), f("fl", 72, 144), A.subtract)
+        cp(t("oBC", 0, 9), f("BC", 0, 9))
+        gat(f("W2", 72, 216), f("W1"), t("oAD", 0, 9))
+        ts(t("oRi", 0, 5), f("BC", 0, 5), -72.0, A.add, 0.0, A.max)
+        gat(f("W3", 72, 216), f("W2"), t("oAD", 0, 9))
+        if r == 0:
+            constants2()
+        gop(f("tw", 0, 16), f("W3"), t("oAD", 0, 1), f("M16n", 0, 16), A.add)
+        gop(f("tw", 16, 32), f("W3"), t("oAD", 8, 9), f("M16n", 0, 16), A.add)
+        def masks():
+            for i in range(4):
+                acts(f("fM4", i, 144, 4), f("fl", i, 144, 4), pcol(16 + i))
+            act(f("fM4", 143, 144), pcol(19))
+            for i in range(2):
+                acts(f("fM2", i, 72, 2), f("fl", i, 72, 2), pcol(20 + i))
+        if r > 0:
+            masks()
+        actg(f("W4", 72, 216), f("W3"), t("oAD", 0, 9))
+        actg(f("W5", 72, 216), f("W3"), t("oAD", 0, 9))
+        if r == 0:
+            masks()
+        def late():
+            actf(f("m144"), f("t16"), IDENT, 0.0, -144.0)
+            actf(f("z4", 0, 216, 6), f("q32", 0, 36), IDENT, 0.0, 0.0)
+            actf(f("z4", 2, 216, 6), f("q32", 0, 36), IDENT, 0.0, 1.0)
+            actf(f("z8", 2, 216, 3), f("t2", 0, 72), IDENT, 0.0, 1.0)
+            actf(f("z8", 0, 216, 24), f("q16", 0, 9), IDENT, 0.0, 0.0)
+            actf(f("m8z"), f("t8"), SIGN, 1.0, 0.0)
+            actf(f("tb", 0, 9), f("cT", 0, 9), IDENT, 2.0, 0.0)
+            actf(f("cc18", 0, 9), f("cT", 0, 9), IDENT, 4.0, 1.0)
+        if r > 0:
+            half_of_xk(1)
+        scan(f("ts"), f("d16", 0, 32), f("tw"), A.min, A.max)
+        cp(t("o4", 0, 4, 2), f("ts", 15, 32, 16))
+        if r > 0:
+            scan(f("fS4"), f("m4z"), f("fM4"), A.mult, A.add)
+        gat(f("W5", 72, 88), f("W4"), t("o4", 0, 1))
+        gat(f("W5", 200, 216), f("W4"), t("o4", 2, 3))
+        if r == 0:
+            scan(f("fS4"), f("m4z"), f("fM4"), A.mult, A.add)
+        tt(f("dj", 0, 36), f("fM2", 0, 72, 2), f("fM2", 1, 72, 2), A.add)
+        gop(f("Vw"), f("W5"), t("oBC", 0, 5), f("M16n", 0, 80), A.add)
+        actg(f("Vb"), f("W5"), t("oBC", 4, 9))
+        ts(f("s1", 0, 36), f("fS4", 3, 144, 4), -2.0, A.mult, 4.0, A.add)
+        scan(f("Vs"), f("d16"), f("Vw"), A.min, A.max)
+        gop(f("Rw"), f("W5"), t("oRi", 0, 5), f("M16n", 0, 80), A.add)
+        ts(t("oVC", 0, 5), f("Vs", 15, 80, 16), -208.0, A.add, 8.0, A.max)
+        scan(f("Rs"), f("d16b", 0, 80), f("Rw"), A.min, A.max)
+        ts(f("fs", 0, 36), f("dj", 0, 36), pcol(9), A.mult, PAR4, A.add)
+        gop(f("Pw"), f("Vb"), t("oVC", 0, 5), f("M16n", 0, 80), A.add)
+        actg(f("F0"), f("Vb"), t("oVC", 0, 5))
+        if r == 0:
+            late()
+        tt(f("x4", 5, 216, 6), f("b1", 0, 36), f("fS4", 3, 144, 4), A.add)
+        scan(f("Ps"), f("d16b", 0, 80), f("Pw"), A.min, A.max)
+        ts(t("oR", 0, 5), f("Rs", 15, 80, 16), 71.0, A.min)
+        table(t("oP0", 0, 5), f("Ps"), 80)
+        low = f("J1")
+        for i in range(4):
+            o = t("oP%d" % i, 0, 5)
+            Fi, Gi, la, lb = f("F%d" % (i % 3)), f("G%d" % (i % 3)), f("l%d" % (2 * i)), f("l%d" % (2 * i + 1))
+            if i < 3:
+                gat(Gi, Fi, o)
+            if i == 0:
+                gop(la, low, o, f("J2"), A.min)
+            else:
+                gop(la, low, o, f("lc"), A.min)
+            if i < 3:
+                gop(f("Gw"), Gi, o, f("M16n", 0, 80), A.add)
+                gop(lb, la, o, low, A.min)
+                if i < 2:
+                    actg(f("F%d" % (i + 1)), Gi, o)
+                act(f("lc"), lb)
+                if r == 0 and i < 2:
+                    actg(t(XK, 2 + i, 1152, 4), t(X), t("k4t0", 40 + 20 * i, 58 + 20 * i), 0.5)
+                if i == (1 if r else 2):
+                    act(t(XC, 0, 576), t(XK, 0, 576))
+                if i == 2:
+                    act(t(XC, 576, 1152), t(XK, 576, 1152))
+                scan(f("Gs"), f("d16b", 0, 80), f("Gw"), A.min, A.max)
+                if i == 0:
+                    tt(f("z4", 5, 216, 6), f("s1", 0, 36), f("fs", 0, 36), A.mult)
+                elif i == 1:
+                    tt(f("f18", 0, 9), sd, f("sgT", 0, 9), A.mult)
+                else:
+                    ts(f("s18", 0, 9), f("f18", 0, 9), -2.0, A.mult, 1.0, A.add)
+                table(t("oP%d" % (i + 1), 0, 5), f("Gs"), 80)
+                if i == 0:
+                    tt(f("fM8", 0, 72), f("fl", 0, 72), f("M8", 0, 72), A.mult)
+                elif i == 1:
+                    tt(f("f18", 8, 9), f("f18", 8, 9), pcol(12), A.max)
+                else:
+                    scan(f("fS8", 0, 72), f("m8z", 0, 72), f("fM8", 0, 72), A.mult, A.add)
+            else:
+                tt(f("x8", 23, 216, 24), f("tb", 0, 9), f("f18", 0, 9), A.add)
+                gop(lb, la, o, f("lc"), A.min)
+            low = lb
+        ts(f("fs18", 0, 9), f("fS8", 7, 72, 8), pcol(10), A.mult, PAR2, A.add)
+        gop(f("x4", 0, 240, 3), low, t("oR", 0, 5), f("JM2"), A.is_equal)
+        tt(f("x4", 1, 216, 3), (low[0], low[1], low[1] + 72, 1), f("JM2", 0, 72), A.is_equal)
+        tt(f("z8", 23, 216, 24), f("fs18", 0, 9), f("s18", 0, 9), A.mult)
+        scan(f("xs4"), f("z4"), f("x4", 0, 216), A.mult, A.add)
+        cp(t("tt4", 0, 36), f("xs4", 5, 216, 6))
+        tt(f("tab2", 0, 36), f("cc4", 0, 36), f("xs4", 5, 216, 6), A.subtract)
+        if r > 0:
+            actg(t(kk), t("kf%d" % r), t(kt), 1.0, -144.0)
+
+        def layer(i, a, b, at):
+            gop(t(Z, 4 * a, 4 * b), t(XK), t("tt4", a // 4, b // 4), t(XC, 4 * a, 4 * b), A.add)
+            if i == 0:
+                cp(t("tt4", 36, 72), f("tab2", 0, 36))
+            n = max(128, b - a)
+            p = 0 if i == 0 else C1 + 128 * (i - 1)
+            q, s = t(zq, p, p + n), t(zs, p, p + n)
+            quant(q, s, t(Z, 4 * (b - n), 4 * b))
+            for k in range(4):
+                mm(bank(at + k, n), t("wq", 128 * k, 128 * k + 128), t("wp", 128 * k, 128 * k + 128), q, s)
+                o, c = bank(at + k, n), t(B, C * k + a, C * k + b) if i == 2 else t(H, 4 * a + k, 4 * b, 4)
+                act(c, (o[0], o[2] - (b - a), o[2], 1), 0.03125)
+
+        layer(0, 0, C1, 4)
+        layer(1, C1, E, 8)
+        quant(t(hq, 0, C1), t(hs, 0, C1), t(H, 0, 4 * C1))
+        dst = partner[r]
+        n = send(dst, "ha%d" % r, t(lq, 0, C1), t(hq, 0, C1), [t(hq, 0, C1)], True)
+        n += send(dst, "ha%d" % r, t(ls, 0, C1), t(hs, 0, C1), [t(hs, 0, C1)])
+        if r == 0:
+            constants3()
+        tt(f("x8", 1, 216, 3), (low[0], low[1], low[1] + 72, 1), f("JM8", 0, 72), A.is_equal)
+        gop(f("x8", 0, 240, 3), low, t("oR", 0, 5), f("JM8"), A.is_equal)
+        quant(t(hq, C1, C1 + 128), t(hs, C1, C1 + 128), t(H, 4 * (E - 128), 4 * E))
+        m = send(dst, "hb%d" % r, t(lq, C1, E), t(hq, C1 + 128 - C2, C1 + 128), [t(hq, C1, C1 + 128)], True)
+        m += send(dst, "hb%d" % r, t(ls, C1, E), t(hs, C1 + 128 - C2, C1 + 128), [t(hs, C1, C1 + 128)])
+        arrives("ha%d" % r, n, [t(lq, 0, C1), t(ls, 0, C1)])
+        arrives("hb%d" % r, m, [t(lq, C1, E), t(ls, C1, E)])
+        scan(f("xs8"), f("z8"), f("x8", 0, 216), A.mult, A.add)
+        layer(2, E, C, 12)
+        if r == 0:
+            constants4()
+        tt(f("up", 0, 9), f("cc18", 0, 9), f("xs8", 23, 216, 24), A.subtract)
+        cp(t("tt18", 0, 9), f("xs8", 23, 216, 24))
+        cp(t("tt18", 9, 18), f("up", 0, 9))
+        if r == 0:
+            ts(t("ki", 0, 18), t("kli"), 15, A.bitwise_and)
+            ts(t("ki", 18, 36), t("kli"), 4, A.arith_shift_right)
+            ts(t("ki", 0, 18), t("ki", 0, 18), 18, A.mult)
+            tt(t("ki", 36, 54), t("ki", 0, 18), t("ki", 18, 36), A.add)
+            cp(t("ks"), t("ki", 36, 54))
+            gop(t(kk), t(kf), t("ks"), f("m144"), A.add)
+        gop(f("n16w"), t(kk), t("tt18"), f("M16n"), A.add)
+        actg(t(nf), t(kk), t("tt18"), 1.0, 144.0)
+        scan(f("n16s"), f("d16b"), f("n16w"), A.min, A.max)
+        ts(t("kt%d" % (r + 1)), f("n16s", 15, 288, 16), 144.0, A.add)
+        if r < 2:
+            for e in range(4):
+                ts(t("k4t%d" % (r + 1), 20 * e, 20 * e + 18), f("n16s", 15, 288, 16), 4.0, A.mult, 576.0 + e, A.add)
+            nd = "nd%d" % (r + 1)
+            dma("y", "dn%d" % (r + 1), T[nd][:, :], T[nf][0:128:16, :], [t(nf)], [t(nd)])
+            lr = "lr%d" % (r + 1)
+            arrives(lr, send(partner[r + 1], lr, t("lk%d" % (r + 1)), t(nd), [t(nd)]), [t("lk%d" % (r + 1))])
+        else:
+            dma("y", "dout", T.kp[:, :], T[nf][0:128:16, :], [t(nf)], [])
+        if r == 0:
+            quant(t("eq"), t("es"), t("et"))
+            quant(t("vq"), t("vs"), t("vb"))
+        for c0, c1, new, at in ((0, C1, 0, 16), (E - 128, E, 128 - C2, 20)):
+            for b in range(4):
+                mm(bank(at + b, c1 - c0), t("eq", 128 * b, 128 * b + 128), t("es", 128 * b, 128 * b + 128), t(lq, c0, c1), t(ls, c0, c1))
+                k = bank(at + b, c1 - c0)
+                k = (k[0], k[1] + new, k[2], 1)
+                act(t(B, C * b + c0 + new, C * b + c1), k)
+        Xn = "X%d" % (r + 1)
+        for e, a, b in ((0, 0, C), (1, 0, C), (2, 0, C), (3, 0, HS[0][1]), (3, HS[1][0], C)):
+            gop(t(Xn, 4 * a + e, 4 * b, 4), t(B, C * e, C * e + C), t("kt%d" % (r + 1), a // 16, b // 16), t(X, 4 * a + e, 4 * b, 4), A.add)
+        for h in range(2):
+            state(r + 1, h)
+            if r < 2:
+                scores(r + 1, h)
+            if r == 2:
+                q, s = "xq3", "xs3"
+                a, b = HS[h]
+                mm(bank(2 + h, b - a), t("vq"), t("vs"), t(q, a, b), t(s, a, b))
+                dma("y", "dout", T.oc[:, 4 * a:4 * b], T[q][:, a:b].bitcast(dt.uint8), [t(q, a, b)], [])
+                for i in range(4):
+                    dma("y", "dout", T.osc[4 * i:4 * i + 4, a:b], T[s][32 * i:32 * i + 4, a:b], [t(s, a, b)], [])
+                act(t("ysb", a, b), bank(2 + h, b - a))
+                dma("s", "dout", T.y[:, a:b], T.ysb[:, a:b], [t("ysb", a, b)], [])
+    need("y", "dout", total["dout"])
+    need("q", "sent", total["sent"])
+    for sem in ("v", "s", "p", "q"):
+        need("y", sem, total[sem])

@@ -7,6 +7,7 @@ HS = ((0, 160), (160, 288))
 C1 = 128
 C2 = E - C1
 F4 = "float8_e4m3fn_x4"
+SEG = 18
 
 SCRATCH = {
     "ub": ("sbuf", [128, 512], "bfloat16"), "vb": ("sbuf", [128, 512], "bfloat16"), "et": ("sbuf", [128, 2048], "bfloat16"),
@@ -21,12 +22,13 @@ SCRATCH = {
     "nd1": ("dram", [128, 18], "float32"), "nd2": ("dram", [128, 18], "float32"),
     "lk1": ("dram", [128, 18], "float32"), "lk2": ("dram", [128, 18], "float32"),
     "kf0": ("sbuf", [128, C], "int32"), "kf1": ("sbuf", [128, C], "float32"), "kf2": ("sbuf", [128, C], "float32"),
-    "pI": ("sbuf", [128, 8], "int32"), "uI": ("sbuf", [128, 8], "int32"), "pF": ("sbuf", [128, 24], "float32"),
-    "uo": ("sbuf", [128, 8], "uint16"),
-    "ks": ("sbuf", [128, 18], "uint16"),
-    "oAD": ("sbuf", [128, 10], "uint16"), "oBC": ("sbuf", [128, 10], "uint16"), "oRi": ("sbuf", [128, 6], "uint16"),
-    "o4": ("sbuf", [128, 4], "uint16"), "oVC": ("sbuf", [128, 6], "uint16"), "oR": ("sbuf", [128, 6], "uint16"),
-    "tt4": ("sbuf", [128, 72], "uint16"), "tt18": ("sbuf", [128, 18], "uint16"),
+    "pI": ("sbuf", [128, 8], "int32"), "uI": ("sbuf", [128, 24], "int32"), "pF": ("sbuf", [128, 24], "float32"),
+    "cI": ("sbuf", [128, 48], "int32"),
+    "uo": ("sbuf", [128, 24], "uint16"), "ks": ("sbuf", [128, 18], "uint16"),
+    "oC": ("sbuf", [128, 16], "uint16"), "oI": ("sbuf", [128, 16], "uint16"),
+    "oA": ("sbuf", [128, 6], "uint16"), "oE": ("sbuf", [128, 4], "uint16"),
+    "oT0": ("sbuf", [128, 10], "uint16"), "oT1": ("sbuf", [128, 6], "uint16"), "oT2": ("sbuf", [128, 6], "uint16"), "oT3": ("sbuf", [128, 6], "uint16"),
+    "tt18": ("sbuf", [128, 18], "uint16"),
     "ps": ("psum", [128, 4096], "float32"),
     "ysb": ("sbuf", [128, C], "float32"),
 }
@@ -34,7 +36,6 @@ for _i in range(4):
     SCRATCH["X%d" % _i] = ("sbuf", [128, 4 * C], "bfloat16")
     SCRATCH["xq%d" % _i] = ("sbuf", [128, C], F4)
     SCRATCH["xs%d" % _i] = ("sbuf", [128, C], "uint8")
-    SCRATCH["oP%d" % _i] = ("sbuf", [128, 6], "uint16")
     SCRATCH["kt%d" % _i] = ("sbuf", [128, 18], "uint16")
 for _i in range(3):
     SCRATCH["XK%d" % _i] = ("sbuf", [128, 4 * C], "bfloat16")
@@ -52,20 +53,19 @@ for _i in range(3):
     SCRATCH["nf%d" % _i] = ("sbuf", [128, C], "float32")
     SCRATCH["kk%d" % _i] = ("sbuf", [128, C], "float32")
 _ROWS = {
-    "t16": 288, "t4": 288, "t8": 80, "t2": 80, "t32": 288, "J1": 80, "J2": 80, "q16": 16, "q32": 40, "m144": 288, "tmp": 288,
-    "W1": 288, "W2": 288, "W3": 288, "W4": 288, "W5": 288, "cAD": 144, "sgM": 144, "M16n": 288, "M4n": 288, "M2": 80, "M8": 80,
-    "m8z": 80, "d16": 80, "JM2": 80, "JM8": 80,
-    "cT": 16, "tA": 16, "tB": 16, "tC": 16, "tD": 16, "tcAD": 16, "tcBC": 16, "sgT": 16, "tb": 16, "cc18": 16,
-    "b1": 40, "cc4": 40, "bits": 288, "fl": 144, "BC": 16, "tw": 32, "ts": 32,
-    "Vw": 80, "Vs": 80, "Vb": 80, "F0": 80, "F1": 80, "F2": 80, "G0": 80, "G1": 80, "G2": 80,
-    "l0": 80, "l1": 80, "l2": 80, "l3": 80, "l4": 80, "l5": 80, "l6": 80, "l7": 80, "lc": 80,
-    "fM2": 80, "dj": 40, "s1": 40, "fs": 40, "x4": 240, "z4": 216, "xs4": 216, "tab2": 40,
-    "fM8": 80, "fS8": 80, "f18": 16, "s18": 16, "fs18": 16, "x8": 240, "z8": 216, "xs8": 216, "up": 16,
+    "t16": 288, "t32": 32, "M16n": 288, "tmp": 288, "pos": 16, "xx": 16, "hb": 96, "hz": 96, "hs": 96, "ww": 16, "t1": 16, "bb": 16,
+    "cf": 16, "a1": 16, "a2": 16, "up": 16, "mem": 32, "rk": 32, "c2": 16, "cb": 16, "cu": 16, "su": 16, "en": 16, "hi": 16, "t8": 80, "e8": 80,
+    "JA": 72, "JB": 144,
 }
 _ROWS2 = {
-    "x2": 288, "z2": 288, "xs2": 288, "n4w": 288, "n4s": 288, "n16w": 288, "n16s": 288, "d4": 288, "d16b": 288,
-    "Pw": 80, "Ps": 80, "Rw": 80, "Rs": 80, "Gw": 80, "Gs": 80, "fM4": 144, "fS4": 144, "m4z": 144,
+    "sg": 288, "fx": 144, "sw": 32, "val": 256, "K": 256, "lk": 192, "lz": 208, "ls": 192, "ek": 64, "ez": 64, "es": 64,
+    "bc": 160, "BT": 160, "M": 288, "MS": 288, "M8": 144,
+    "sf": 288, "wv": 288, "Fa": 160, "Fb": 160, "Fc": 160, "RD": 128, "La": 160, "Lb": 160, "Lc": 160, "Ld": 160,
+    "ts": 160, "rs": 128, "fc": 288, "fj": 144, "J": 80, "x": 288, "z": 288, "xs": 288,
+    "n16w": 288, "n16s": 288, "d16b": 288,
 }
+_ROW_OF = {"F1": "Fa", "F2": "Fb", "F3": "Fc", "F4": "Fa", "F7": "Fb", "F10": "Fc", "F17": "Fa", "L2": "La", "L3": "Lb", "L4": "Lc",
+           "L7": "La", "L10": "Ld", "L17": "Lc", "L24": "Lb", "L41": "Ld", "L58": "La", "L75": "Lb"}
 OFF = {}
 for _b, _t, _d in (("F", _ROWS, "float32"), ("G", _ROWS2, "bfloat16")):
     _n = 0
@@ -75,7 +75,7 @@ for _b, _t, _d in (("F", _ROWS, "float32"), ("G", _ROWS2, "bfloat16")):
     SCRATCH[_b] = ("sbuf", [128, _n], _d)
 
 SEMAPHORES = ["v", "s", "p", "q", "sent", "dx0", "dx1", "dk", "du", "dw", "dv", "dkl", "dn1", "dn2", "df0", "df1", "df2", "dout",
-              "lr0", "lr1", "lr2", "ha0", "ha1", "ha2", "hb0", "hb1", "hb2"]
+              "lr0", "lr1", "lr2", "ha0", "ha1", "ha2", "hb0", "hb1", "hb2", "dc0", "dc1", "dc2", "dd0", "dd1", "dd2"]
 
 
 def rank_program(g, core, T, topo):
@@ -88,7 +88,7 @@ def rank_program(g, core, T, topo):
     total, known, log = {}, {}, {}
 
     def f(name, a=0, b=None, step=1):
-        o = OFF[name]
+        o = OFF[_ROW_OF.get(name, name)]
         return (o[0], o[1] + a, o[1] + (o[2] if b is None else b), step)
 
     def t(name, a=0, b=None, step=1):
@@ -103,7 +103,7 @@ def rank_program(g, core, T, topo):
     def clash(x, y):
         if x[0] != y[0] or x[1] >= y[2] or y[1] >= x[2]:
             return False
-        if x[3] == y[3] and x[3] > 1 and (x[1] - y[1]) % x[3]:
+        if x[3] > 1 and y[3] > 1 and (x[3] % y[3] == 0 or y[3] % x[3] == 0) and (x[1] - y[1]) % min(x[3], y[3]):
             return False
         return True
 
@@ -146,14 +146,15 @@ def rank_program(g, core, T, topo):
     def tt(out, a, b, op):
         run("v", lambda: g.vector.tensor_tensor(ap(out), ap(a), ap(b), op), [a, b], [out])
 
-    def ts(out, a, s1, op0, s2=None, op1=None):
-        sc = [x for x in (s1, s2) if isinstance(x, tuple)]
+    def ts(out, a, s1, op0, s2=None, op1=None, off=None):
+        sc = [x for x in (s1, s2, off) if isinstance(x, tuple)]
         u1 = ap(s1) if isinstance(s1, tuple) else s1
         u2 = ap(s2) if isinstance(s2, tuple) else s2
+        src = ap(a) if off is None else ind(a, off)
         if op1 is None:
-            run("v", lambda: g.vector.tensor_scalar(ap(out), ap(a), u1, None, op0), [a] + sc, [out])
+            run("v", lambda: g.vector.tensor_scalar(ap(out), src, u1, None, op0), [a] + sc, [out])
         else:
-            run("v", lambda: g.vector.tensor_scalar(ap(out), ap(a), u1, u2, op0, op1), [a] + sc, [out])
+            run("v", lambda: g.vector.tensor_scalar(ap(out), src, u1, u2, op0, op1), [a] + sc, [out])
 
     def cp(out, a):
         run("v", lambda: g.vector.tensor_copy(ap(out), ap(a)), [a], [out])
@@ -164,14 +165,11 @@ def rank_program(g, core, T, topo):
     def gop(out, win, off, b, op):
         run("v", lambda: g.vector.tensor_tensor(ap(out), ind(win, off), ap(b), op), [win, off, b], [out])
 
-    def scan(out, d0, d1, op0, op1):
-        run("v", lambda: g.vector.tensor_tensor_scan(ap(out), ap(d0), ap(d1), 0.0, op0, op1), [d0, d1], [out])
+    def scan(out, d0, d1, op0, op1, first=0.0):
+        run("v", lambda: g.vector.tensor_tensor_scan(ap(out), ap(d0), ap(d1), first, op0, op1), [d0, d1], [out])
 
     def act(out, a, scale=1.0):
         run("s", lambda: g.scalar.activation(ap(out), ap(a), COPY, scale=scale), [a], [out])
-
-    def acts(out, a, col):
-        run("s", lambda: g.scalar.activation(ap(out), ap(a), COPY, scale=ap(col)), [a, col], [out])
 
     def actf(out, a, func, scale, bias):
         if isinstance(bias, tuple):
@@ -199,7 +197,7 @@ def rank_program(g, core, T, topo):
         run("p", lambda: g.tensor.matmul_mx(ap(out), ap(l), ap(ls), ap(r), ap(rs), True, True), [l, ls, r, rs], [out])
 
     def iota(out, pattern, base=0, cm=0):
-        if out[0] == "F":
+        if out[0] in "FG":
             run("q", lambda: g.iota(ap(out), pattern, base, cm, allow_small_or_imprecise_dtypes=True), [], [out])
         else:
             run("q", lambda: g.iota(ap(out), pattern, base, cm), [], [out])
@@ -234,52 +232,98 @@ def rank_program(g, core, T, topo):
     dma("y", "dv", T.vb[:, :], T.v[:, :], [], [t("vb")])
 
     iota(t("pI", 0, 1), [[0, 1]], 0, 1)
-    iota(t("uI"), [[16, 8]])
+    iota(t("uI", 0, 12), [[16, 12]])
+    iota(f("bb", 12, 16), [[-1, 4]], 3)
+    iota(t("uI", 12, 22), [[SEG, 5], [0, 2]], 6 * SEG - 1)
+    iota(f("up", 12, 16), [[0, 4]], 1)
+    iota(f("t32"), [[1, 32]])
+    for k in range(4):
+        iota(f("rk", 16 >> k, 32 >> k), [[0, 16 >> k]], 8 >> k)
+    iota(f("wv", 128, 288, 2), [[-64, 5], [-2, 16]], 286)
+    iota(f("sw", 0, 32, 16), [[-2, 2]], 1)
+    iota(f("wv", 0, 144, 2), [[4, 72]])
     iota(f("t16"), [[0, 18], [1, 16]])
-    iota(f("q16", 0, 9), [[16, 9]])
-    iota(f("t32"), [[0, 9], [1, 32]])
-    iota(f("t2"), [[0, 40], [1, 2]])
+    iota(f("fx"), [[0, 144]], -1)
+    iota(f("lz", 0, 11 * SEG), [[0, 11], [512, SEG]])
     iota(f("t8"), [[0, 10], [1, 8]])
-    iota(f("J1"), [[1, 80]], 1)
-    iota(f("q32", 0, 36), [[32, 36]])
-    for i, base in enumerate((72, 216, 1, 145)):
-        iota(f("cAD", 36 * i, 36 * i + 36), [[2, 36]], base)
-    iota(f("W1"), [[1, 288]])
-    iota(f("t4"), [[0, 72], [1, 4]])
+    iota(f("ez"), [[0, 4], [512, 16]])
+    iota(f("J"), [[2, 80]])
     partner = [T.cores[rank ^ m] for m in MASKS]
     arrives("lr0", send(partner[0], "lr0", t("lk0"), t("kld"), [t("kld")]), [t("lk0")])
+    iota(f("JB"), [[256, 9], [17, 16]])
+    iota(f("JA"), [[256, 9], [33, 8]])
+    for a, step, c in ((0, 4, 1), (1, 4, -1), (2, 4, -1), (3, 4, 1), (0, 32, 0)):
+        iota(f("z", a, 288, step), [[0, 288 // step]], c)
+    iota(f("x", 3, 288, 4), [[0, 72]])
+    iota(f("d16b"), [[0, 18], [16384, 16]], -8192)
 
     def pcol(i):
         return t("pF", i, i + 1)
 
-    cp(t("uo"), t("uI"))
+    fill(("G", OFF["sf"][1] + 1, OFF["ts"][1], 2), 0.0)
+    fill(f("hz"), 2.0)
     ts(t("pI", 1, 2), t("pI", 0, 1), 15, A.bitwise_and)
-    ts(t("pI", 2, 3), t("pI", 0, 1), 3, A.bitwise_and)
-    ts(t("pI", 3, 4), t("pI", 0, 1), 15, A.bitwise_and, 2, A.arith_shift_right)
-    ts(t("pI", 4, 5), t("pI", 0, 1), 15, A.bitwise_and, 3, A.arith_shift_right)
-    ts(t("pI", 5, 6), t("pI", 0, 1), 15, A.bitwise_and, 1, A.arith_shift_right)
-    ts(t("pI", 6, 7), t("pI", 0, 1), 2, A.arith_shift_right, 1, A.bitwise_and)
-    ts(t("pI", 7, 8), t("pI", 0, 1), 1, A.bitwise_and)
-    cp(t("pF", 0, 8), t("pI"))
-    P16, P4, I4, I8, I2, PAR4, PAR2 = [pcol(i) for i in range(1, 8)]
+    ts(t("pI", 2, 3), t("pI", 0, 1), 16, A.bitwise_and)
+    ts(t("pI", 3, 4), t("pI", 0, 1), 14, A.bitwise_and)
+    ts(t("pI", 4, 5), t("pI", 0, 1), 1, A.bitwise_and)
+    fill(f("hz", 0, 96, 6), 0.0)
+    cp(t("pF", 1, 5), t("pI", 1, 5))
+    P16, ODD16, P14, PAR = [pcol(i) for i in range(1, 5)]
+    cp(t("uo", 0, 22), t("uI", 0, 22))
+    ts(f("pos", 0, 12), t("uI", 0, 12), P16, A.add)
+    actf(pcol(5), P16, IDENT, -0.125, 3.875)
+    actf(pcol(6), P16, IDENT, 1.0, 2.0)
+    actf(pcol(9), P14, IDENT, 0.5, 0.0)
+    actf(f("xx", 12, 16), f("bb", 12, 16), IDENT, 0.0, pcol(6))
+    actf(pcol(14), PAR, IDENT, -2.0, 1.0)
+    actf(f("cb", 0, 9), f("pos", 0, 9), IDENT, 2.0, -147.5)
+    actf(f("cu", 0, 9), f("pos", 0, 9), IDENT, 4.0, -143.0)
+    actf(pcol(15), pcol(14), IDENT, -4.0, 0.5)
+    ts(t("cI", 16, 28), f("pos", 0, 12), 1.0 / SEG, A.mult, -0.47, A.add)
+    ts(f("a1", 0, 12), t("cI", 16, 28), float(-SEG), A.mult)
+    ts(f("a2", 0, 12), t("cI", 16, 28), 5.0, A.is_ge, 5.0, A.mult)
+    ts(f("bb", 0, 12), t("cI", 16, 28), -1.0, A.mult, 8.0, A.add)
+    tt(f("xx", 0, 12), f("a1", 0, 12), f("pos", 0, 12), A.add)
+    ts(f("up", 0, 12), t("cI", 16, 28), 5.0, A.is_lt)
+    tt(f("bb", 0, 12), f("bb", 0, 12), f("a2", 0, 12), A.add)
+    for k, th in enumerate((10.0, 6.0, 4.0, 3.0, 2.0, 1.0)):
+        ts(f("hb", k, 96, 6), f("xx"), th, A.is_ge)
+    ts(f("t1"), f("xx"), -2.0, A.add, 0.0, A.max)
+    ts(t("ki", 2, 32), f("rk", 2, 32), pcol(5), A.mult, -0.47, A.add)
+    scan(f("hs"), f("hz"), f("hb"), A.mult, A.add)
+    tt(f("bb"), f("bb"), f("hb", 3, 96, 6), A.subtract)
+    tt(f("mem", 2, 32), t("ki", 2, 32), f("t32", 2, 32), A.is_equal)
+    ts(f("ww"), f("hs", 5, 96, 6), 1.0, A.add, 0.125, A.mult)
+    ts(t("k4t0", 20, 38), t("kli"), 4, A.mult, 1, A.add)
+    tt(f("sw", 1, 16), f("mem", 2, 32, 2), f("mem", 3, 32, 2), A.subtract)
+    tt(f("cf"), f("ww"), f("bb"), A.mult)
+    ts(t("k4t0", 40, 58), t("kli"), 4, A.mult, 2, A.add)
+    tt(f("cf"), f("cf"), f("t1"), A.add)
+    ts(t("k4t0", 60, 78), t("kli"), 4, A.mult, 3, A.add)
+    ts(t("cI", 0, 16), f("cf"), -0.44, A.add)
+    ts(t("cI", 32, 48), f("cf"), 2.0, A.mult, -0.44, A.add)
+    ts(t("k4t0", 0, 18), t("kli"), 4, A.mult, 0, A.add)
+    cp(t("kt0"), t("kli"))
+    quant(t("uq"), t("us"), t("ub"))
+    ts(f("a1"), t("cI", 0, 16), -4.0, A.mult, 286.0, A.add)
+    ts(f("a2"), t("cI", 0, 16), 2.0, A.mult)
+    run("v", lambda: g.vector.tensor_copy(T.ur[:, 0:128].bitcast(dt.uint32), T.uq[:, 0:128].bitcast(dt.uint32).indirect(T.uo[:, 0:8])),
+        [t("uq"), t("uo")], [t("ur")])
     equal(f("M16n"), f("t16"), P16, f("tmp"))
-    act(f("sgM", 0, 72), f("M16n", 0, 72))
-    act(f("sgM", 72, 144), f("M16n", 72, 144), -1.0)
-    actf(f("z2"), f("t32"), SIGN, 1.0, 0.0)
-    actf(f("d16"), f("t16", 0, 80), SIGN, 1.0, 0.0)
-    fill(f("x2"), 0.0)
-    ts(f("cT", 0, 9), f("q16", 0, 9), P16, A.add)
-    ts(f("tA", 0, 9), f("cT", 0, 9), 36.0, A.is_ge, 72.0, A.mult)
-    ts(f("tB", 0, 9), f("cT", 0, 9), 108.0, A.is_ge, 72.0, A.mult)
-    ts(f("tC", 0, 9), f("cT", 0, 9), 72.0, A.is_ge, 287.0, A.mult)
-    ts(f("tD", 0, 9), f("cT", 0, 9), 2.0, A.mult, 72.0, A.add)
-    tt(f("tA", 0, 9), f("tA", 0, 9), f("tB", 0, 9), A.add)
-    tt(f("tD", 0, 9), f("tD", 0, 9), f("tC", 0, 9), A.subtract)
-    ts(f("sgT", 0, 9), f("cT", 0, 9), 72.0, A.is_ge, -2.0, A.mult)
-    ts(f("sgT", 0, 9), f("sgT", 0, 9), 1.0, A.add)
-    tt(f("tcAD", 0, 9), f("tA", 0, 9), f("tD", 0, 9), A.add)
-    tt(f("tcBC", 0, 9), f("tcAD", 0, 9), f("sgT", 0, 9), A.add)
-    ts(f("x2", 31, 288, 32), f("tcAD", 0, 9), -144.0, A.add)
+    run("s", lambda: g.scalar.activation(T.urs[:, 0:128], T.us[:, 0:128].indirect(T.uo[:, 0:8]), COPY), [t("us"), t("uo")], [t("urs")])
+    tt(f("a1"), f("a1"), f("up"), A.mult)
+    tt(f("c2"), t("cI", 32, 48), f("a2"), A.subtract)
+    tt(f("a1"), f("a1"), f("a2"), A.add)
+    ts(f("c2"), f("c2"), 16.0, A.mult)
+    cp(t("oC"), f("a1"))
+    tt(f("c2"), f("c2"), f("t1"), A.add)
+    actg(f("val"), f("wv"), t("oC"))
+    act(f("M", 0, 288, 2), f("M16n", 0, 144), 256.0)
+    act(f("M", 1, 288, 2), f("M16n", 1, 145), -4096.0)
+    equal(f("e8"), f("t8"), pcol(9), f("tmp", 0, 80))
+    act(f("MS"), f("M"), 1.0 / 64)
+    act(f("M8", 0, 144, 2), f("e8", 0, 72), 4.0)
+    act(f("M8", 1, 144, 2), f("e8", 1, 73), -64.0)
 
     def state(r, h):
         a, b = HS[h]
@@ -289,200 +333,120 @@ def rank_program(g, core, T, topo):
         a, b = HS[h]
         mm(bank(2 + h, b - a), t("ur"), t("urs"), t("xq%d" % r, a, b), t("xs%d" % r, a, b))
 
-    fill(f("x4"), 0.0)
-    fill(f("z4"), -1.0)
-    fill(f("x8"), 0.0)
-    fill(f("z8"), -1.0)
-    quant(t("uq"), t("us"), t("ub"))
     state(0, 0)
+    cp(t("oI"), f("c2"))
     state(0, 1)
-    run("v", lambda: g.vector.tensor_copy(T.ur[:, 0:128].bitcast(dt.uint32), T.uq[:, 0:128].bitcast(dt.uint32).indirect(T.uo[:, 0:8])),
-        [t("uq"), t("uo")], [t("ur")])
-    run("s", lambda: g.scalar.activation(T.urs[:, 0:128], T.us[:, 0:128].indirect(T.uo[:, 0:8]), COPY), [t("us"), t("uo")], [t("urs")])
-
-    def ends(n):
-        act(f(n, 0, 72), f("W1", 0, 72))
-        act(f(n, 216, 288), f("W1", 216, 288))
-
-    actf(f("d16"), f("d16"), IDENT, 16384.0, -8192.0)
-    actf(f("M16n"), f("M16n"), IDENT, 4096.0, -4096.0)
-    ends("W2")
-    act(f("d16b", 0, 80), f("d16"))
-    ends("W3")
-    act(f("J2"), f("J1"))
-
     scores(0, 0)
     scores(0, 1)
-    cp(t("kt0"), t("kli"))
-    for e in range(4):
-        ts(t("k4t0", 20 * e, 20 * e + 18), t("kli"), 4, A.mult, e, A.add)
-    run("v", lambda: g.vector.memset(T.one[:, 0:512], 1.0), [], [t("one")])
+    fill(f("fx", 143, 144), 0.5)
+    gop(f("K"), f("sw", 0, 17), t("oI"), f("val"), A.mult)
+    run("q", lambda: g.iota(T.one[:, 0:512], [[0, 512]], 1, 0, allow_small_or_imprecise_dtypes=True), [], [t("one")])
     for e in range(4):
         run("q", lambda: g.affine_select(T.et[:, 512 * e:512 * e + 512], T.one[:, 0:512], [[-1, 512]], A.is_equal, 0.0, e, 4),
             [t("one")], [t("et", 512 * e, 512 * e + 512)])
 
-    def constants2():
-        ts(t("pF", 16, 20), f("t4", 0, 4), I4, A.is_equal, 4.0, A.mult)
-        ts(t("pF", 20, 22), f("t4", 0, 2), I8, A.is_equal)
-        ts(t("pF", 9, 11), t("pF", 6, 8), -2.0, A.mult, 1.0, A.add)
-        ts(pcol(13), I4, 0.0, A.is_equal)
-        ts(pcol(8), I4, 8.0, A.mult, P4, A.add)
-        ts(pcol(12), P16, 15.0, A.is_equal)
-        tt(f("JM2"), f("J1"), f("M2"), A.mult)
-        tt(f("JM2", 0, 1), f("JM2", 0, 1), pcol(13), A.subtract)
-        actf(f("b1", 0, 36), f("q32", 0, 36), IDENT, 1.0, pcol(8))
-        actf(f("cc4", 0, 36), f("b1", 0, 36), IDENT, 2.0, 4.0)
+    def marks():
+        actf(pcol(10), P16, IDENT, -1.0 / 16, pcol(14))
+        actf(pcol(11), pcol(9), IDENT, -1.0 / 16, 0.0)
+        actf(pcol(12), f("M16n", 0, 1), IDENT, -0.5, 0.0)
+        actf(pcol(10), pcol(10), IDENT, 1.0, PAR)
+        actf(f("JA"), f("JA"), IDENT, 1.0 / 16, pcol(11))
+        actf(pcol(10), pcol(10), IDENT, 1.0, -1.0)
+        actf(f("JA", 0, 1), f("JA", 0, 1), IDENT, 1.0, pcol(12))
+        actf(f("JB"), f("JB"), IDENT, 1.0 / 16, pcol(10))
+        actf(f("M16n"), f("M16n"), IDENT, 4096.0, -4096.0)
+        actf(f("JB", 0, 1), f("JB", 0, 1), IDENT, 1.0, pcol(12))
 
-    def constants3():
-        ts(pcol(14), P16, 0.0, A.is_equal)
-        tt(f("JM8"), f("J1"), f("M8"), A.mult)
-        tt(f("JM8", 0, 1), f("JM8", 0, 1), pcol(14), A.subtract)
+    def even(n):
+        return f(n, 0, 160, 2)
 
-    def constants4():
-        ts(f("tmp"), f("t16"), 0.0, A.is_gt, 16384.0, A.mult)
-        ts(f("d16b"), f("tmp"), -8192.0, A.add)
+    def table(i, row):
+        scan(f("ts"), f(row), f("M", 0, 160), A.max, A.add, -4096.0)
+        return lambda: ts(t("oT%d" % i, 0, 5), f("ts", 30, 160, 32), -256.0, A.add)
 
-    def table(out, src, n, step=16):
-        cp(out, (src[0], src[1] + step - 1, src[1] + n, step))
+    def lowest(out, win, i, other):
+        gop(even(out), f(win), t("oT%d" % i, 0, 5), other if isinstance(other, tuple) else even(other), A.min)
 
     for r in range(3):
         X, XK, XC, Z, H, B, kt = ["%s%d" % (n, r) for n in ("X", "XK", "XC", "Z", "H", "B", "kt")]
         zq, zs, hq, hs, lq, ls, nf, kk = ["%s%d" % (n, r) for n in ("zq", "zs", "hq", "hs", "lq", "ls", "nf", "kk")]
         kf, lk = "kf%d" % r, "lk%d" % r
+
+        def xk(e):
+            actg(t(XK, C * e, C * e + C), t(X), t("k4t%d" % r, 20 * e, 20 * e + 18), 0.5)
+            if e % 2:
+                a, b = C * (e - 1), C * (e + 1)
+                dma("y", "d%s%d" % ("cd"[e // 2], r), T[XC][:, a:b], T[XK][:, a:b], [t(XK, a, b)], [t(XC, a, b)])
+
+        xk(0)
+        xk(1)
+        for h in range(2):
+            ts(f("sg", HS[h][0], HS[h][1]), bank(2 + h, HS[h][1] - HS[h][0]), 0.0, A.is_gt, -0.5, A.add)
+        if r:
+            xk(2)
+        gop(f("sf", 0, 288, 2), f("sg"), t(kt, 0, 9), f("fx"), A.max)
+        gop(f("lk"), f("sf"), t("oC", 0, 12), f("K", 0, 192), A.mult)
+        scan(f("ls"), f("lz", 0, 192), f("lk"), A.min, A.max)
+        gop(f("ek"), f("sf"), t("oC", 12, 16), f("K", 192, 256), A.mult)
+        actg(f("bc"), f("ls"), t("uo", 12, 22))
+        xk(3 if r else 2)
+        ts(t("oA", 0, 5), f("ls", SEG - 1, 5 * SEG, SEG), ODD16, A.add)
+        scan(f("es"), f("ez"), f("ek"), A.min, A.max)
+        scan(f("fc"), f("sf"), f("MS"), A.max, A.add, -64.0)
+        ts(t("oE"), f("es", 15, 64, 16), ODD16, A.add)
+        run("v", lambda: g.vector.transpose(ap(f("BT")), ap(f("bc"))), [f("bc")], [f("BT")])
+        scan(f("fj"), f("sf", 0, 144), f("M8"), A.max, A.add, -64.0)
+        gat(even("F1"), f("BT"), t("oA", 0, 5))
+        gop(even("L2"), f("BT"), t("oA", 0, 5), f("J"), A.min)
+        end = table(0, "F1")
+        ts(f("su", 0, 9), f("fc", 30, 288, 32), -4.0, A.add, 2.0, A.mult)
+        end()
+        actg(f("RD", 0, 128, 2), f("BT"), t("oE"))
+        if r == 0:
+            xk(3)
         for i in range(16):
             dma("y", "df%d" % r, T[kf][i:128:16, :], T[lk][:, :], [t(lk)], [(kf, i, C, 16)])
-        for h in range(2):
-            ts(f("bits", HS[h][0], HS[h][1]), bank(2 + h, HS[h][1] - HS[h][0]), 0.0, A.is_gt)
-        actg(f("fl"), f("bits"), t(kt, 0, 9))
-
-        def half_of_xk(h):
-            for e in (2 * h, 2 * h + 1):
-                actg(t(XK, e, 1152, 4), t(X), t("k4t%d" % r, 20 * e, 20 * e + 18), 0.5)
-
-        half_of_xk(0)
+        actg(even("F2"), f("F1"), t("oT0", 0, 5))
+        actg(even("F3"), f("F2"), t("oT0", 0, 5))
+        lowest("L3", "L2", 0, f("J"))
+        tt(f("x", 31, 288, 32), f("fc", 30, 288, 32), f("cb", 0, 9), A.add)
+        lowest("L4", "L3", 0, f("J"))
+        scan(f("rs"), f("RD"), f("M", 0, 128), A.max, A.add, -4096.0)
+        end = table(1, "F3")
+        actg(even("F4"), f("F3"), t("oT0", 0, 5))
+        ts(f("en", 0, 9), f("fj", 14, 144, 16), pcol(14), A.mult, pcol(15), A.add)
+        end()
+        actg(even("F7"), f("F4"), t("oT1", 0, 5))
+        tt(f("z", 31, 288, 32), f("su", 0, 9), f("en", 0, 9), A.mult)
+        lowest("L7", "L4", 1, "L3")
+        end = table(2, "F7")
+        actg(even("F10"), f("F7"), t("oT1", 0, 5))
+        lowest("L10", "L7", 1, "L3")
+        end()
+        actg(even("F17"), f("F10"), t("oT2", 0, 5))
+        lowest("L17", "L10", 2, "L7")
+        end = table(3, "F17")
+        lowest("L24", "L17", 2, "L7")
+        end()
         if r == 0:
-            ends("W4")
-            ends("W5")
-            for m, c, i, o in (("M2", "t2", I8, 0), ("M8", "t8", I2, 80)):
-                equal(f(m), f(c), i, f("tmp", o, o + 80))
-            actf(f("m4z"), f("t4", 0, 144), SIGN, 1.0, 0.0)
-        gop(f("x2", 0, 288, 2), f("bits"), t(kt, 0, 9), f("sgM"), A.mult)
-        scan(f("xs2"), f("z2"), f("x2"), A.mult, A.add)
-        sd = f("xs2", 30, 288, 32)
-        ts(t("oAD", 0, 9), f("xs2", 31, 288, 32), 144.0, A.add)
-        tt(f("BC", 0, 9), f("tcBC", 0, 9), sd, A.subtract)
-        tt(f("W1", 72, 144), f("cAD", 0, 72), f("fl", 0, 72), A.add)
-        tt(f("W1", 144, 216), f("cAD", 72, 144), f("fl", 72, 144), A.subtract)
-        cp(t("oBC", 0, 9), f("BC", 0, 9))
-        gat(f("W2", 72, 216), f("W1"), t("oAD", 0, 9))
-        ts(t("oRi", 0, 5), f("BC", 0, 5), -72.0, A.add, 0.0, A.max)
-        gat(f("W3", 72, 216), f("W2"), t("oAD", 0, 9))
-        if r == 0:
-            constants2()
-        gop(f("tw", 0, 16), f("W3"), t("oAD", 0, 1), f("M16n", 0, 16), A.add)
-        gop(f("tw", 16, 32), f("W3"), t("oAD", 8, 9), f("M16n", 0, 16), A.add)
-        def masks():
-            for i in range(4):
-                acts(f("fM4", i, 144, 4), f("fl", i, 144, 4), pcol(16 + i))
-            act(f("fM4", 143, 144), pcol(19))
-            for i in range(2):
-                acts(f("fM2", i, 72, 2), f("fl", i, 72, 2), pcol(20 + i))
-        if r > 0:
-            masks()
-        actg(f("W4", 72, 216), f("W3"), t("oAD", 0, 9))
-        actg(f("W5", 72, 216), f("W3"), t("oAD", 0, 9))
-        if r == 0:
-            masks()
-        def late():
-            actf(f("m144"), f("t16"), IDENT, 0.0, -144.0)
-            actf(f("z4", 0, 216, 6), f("q32", 0, 36), IDENT, 0.0, 0.0)
-            actf(f("z4", 2, 216, 6), f("q32", 0, 36), IDENT, 0.0, 1.0)
-            actf(f("z8", 2, 216, 3), f("t2", 0, 72), IDENT, 0.0, 1.0)
-            actf(f("z8", 0, 216, 24), f("q16", 0, 9), IDENT, 0.0, 0.0)
-            actf(f("m8z"), f("t8"), SIGN, 1.0, 0.0)
-            actf(f("tb", 0, 9), f("cT", 0, 9), IDENT, 2.0, 0.0)
-            actf(f("cc18", 0, 9), f("cT", 0, 9), IDENT, 4.0, 1.0)
-        if r > 0:
-            half_of_xk(1)
-        scan(f("ts"), f("d16", 0, 32), f("tw"), A.min, A.max)
-        cp(t("o4", 0, 4, 2), f("ts", 15, 32, 16))
-        if r > 0:
-            scan(f("fS4"), f("m4z"), f("fM4"), A.mult, A.add)
-        gat(f("W5", 72, 88), f("W4"), t("o4", 0, 1))
-        gat(f("W5", 200, 216), f("W4"), t("o4", 2, 3))
-        if r == 0:
-            scan(f("fS4"), f("m4z"), f("fM4"), A.mult, A.add)
-        tt(f("dj", 0, 36), f("fM2", 0, 72, 2), f("fM2", 1, 72, 2), A.add)
-        gop(f("Vw"), f("W5"), t("oBC", 0, 5), f("M16n", 0, 80), A.add)
-        actg(f("Vb"), f("W5"), t("oBC", 4, 9))
-        ts(f("s1", 0, 36), f("fS4", 3, 144, 4), -2.0, A.mult, 4.0, A.add)
-        scan(f("Vs"), f("d16"), f("Vw"), A.min, A.max)
-        gop(f("Rw"), f("W5"), t("oRi", 0, 5), f("M16n", 0, 80), A.add)
-        ts(t("oVC", 0, 5), f("Vs", 15, 80, 16), -208.0, A.add, 8.0, A.max)
-        scan(f("Rs"), f("d16b", 0, 80), f("Rw"), A.min, A.max)
-        ts(f("fs", 0, 36), f("dj", 0, 36), pcol(9), A.mult, PAR4, A.add)
-        gop(f("Pw"), f("Vb"), t("oVC", 0, 5), f("M16n", 0, 80), A.add)
-        actg(f("F0"), f("Vb"), t("oVC", 0, 5))
-        if r == 0:
-            late()
-        tt(f("x4", 5, 216, 6), f("b1", 0, 36), f("fS4", 3, 144, 4), A.add)
-        scan(f("Ps"), f("d16b", 0, 80), f("Pw"), A.min, A.max)
-        ts(t("oR", 0, 5), f("Rs", 15, 80, 16), 71.0, A.min)
-        table(t("oP0", 0, 5), f("Ps"), 80)
-        low = f("J1")
-        for i in range(4):
-            o = t("oP%d" % i, 0, 5)
-            Fi, Gi, la, lb = f("F%d" % (i % 3)), f("G%d" % (i % 3)), f("l%d" % (2 * i)), f("l%d" % (2 * i + 1))
-            if i < 3:
-                gat(Gi, Fi, o)
-            if i == 0:
-                gop(la, low, o, f("J2"), A.min)
-            else:
-                gop(la, low, o, f("lc"), A.min)
-            if i < 3:
-                gop(f("Gw"), Gi, o, f("M16n", 0, 80), A.add)
-                gop(lb, la, o, low, A.min)
-                if i < 2:
-                    actg(f("F%d" % (i + 1)), Gi, o)
-                act(f("lc"), lb)
-                if r == 0 and i < 2:
-                    actg(t(XK, 2 + i, 1152, 4), t(X), t("k4t0", 40 + 20 * i, 58 + 20 * i), 0.5)
-                if i == (1 if r else 2):
-                    act(t(XC, 0, 576), t(XK, 0, 576))
-                if i == 2:
-                    act(t(XC, 576, 1152), t(XK, 576, 1152))
-                scan(f("Gs"), f("d16b", 0, 80), f("Gw"), A.min, A.max)
-                if i == 0:
-                    tt(f("z4", 5, 216, 6), f("s1", 0, 36), f("fs", 0, 36), A.mult)
-                elif i == 1:
-                    tt(f("f18", 0, 9), sd, f("sgT", 0, 9), A.mult)
-                else:
-                    ts(f("s18", 0, 9), f("f18", 0, 9), -2.0, A.mult, 1.0, A.add)
-                table(t("oP%d" % (i + 1), 0, 5), f("Gs"), 80)
-                if i == 0:
-                    tt(f("fM8", 0, 72), f("fl", 0, 72), f("M8", 0, 72), A.mult)
-                elif i == 1:
-                    tt(f("f18", 8, 9), f("f18", 8, 9), pcol(12), A.max)
-                else:
-                    scan(f("fS8", 0, 72), f("m8z", 0, 72), f("fM8", 0, 72), A.mult, A.add)
-            else:
-                tt(f("x8", 23, 216, 24), f("tb", 0, 9), f("f18", 0, 9), A.add)
-                gop(lb, la, o, f("lc"), A.min)
-            low = lb
-        ts(f("fs18", 0, 9), f("fS8", 7, 72, 8), pcol(10), A.mult, PAR2, A.add)
-        gop(f("x4", 0, 240, 3), low, t("oR", 0, 5), f("JM2"), A.is_equal)
-        tt(f("x4", 1, 216, 3), (low[0], low[1], low[1] + 72, 1), f("JM2", 0, 72), A.is_equal)
-        tt(f("z8", 23, 216, 24), f("fs18", 0, 9), f("s18", 0, 9), A.mult)
-        scan(f("xs4"), f("z4"), f("x4", 0, 216), A.mult, A.add)
-        cp(t("tt4", 0, 36), f("xs4", 5, 216, 6))
-        tt(f("tab2", 0, 36), f("cc4", 0, 36), f("xs4", 5, 216, 6), A.subtract)
-        if r > 0:
-            actg(t(kk), t("kf%d" % r), t(kt), 1.0, -144.0)
+            marks()
+        else:
+            actg(t(kk), t(kf), t(kt), 1.0, -144.0)
+        ts(t("oT0", 5, 9), f("rs", 30, 128, 32), -256.0, A.add)
+        lowest("L41", "L24", 3, "L17")
+        lowest("L58", "L41", 3, "L17")
+        lowest("L75", "L58", 3, "L17")
+        gop(f("x", 0, 288, 2), f("L75"), t("oT0", 0, 9), f("JB"), A.is_equal)
+        tt(f("x", 1, 288, 4), f("L75", 0, 144, 2), f("JA", 0, 72), A.is_equal)
+        scan(f("xs"), f("z"), f("x"), A.mult, A.add)
+        ts(t("tt18", 0, 9), f("xs", 31, 288, 32), 144.0, A.add)
+        tt(f("hi", 0, 9), f("cu", 0, 9), f("xs", 31, 288, 32), A.subtract)
 
         def layer(i, a, b, at):
-            gop(t(Z, 4 * a, 4 * b), t(XK), t("tt4", a // 4, b // 4), t(XC, 4 * a, 4 * b), A.add)
-            if i == 0:
-                cp(t("tt4", 36, 72), f("tab2", 0, 36))
+            for e in range(4):
+                gop(t(Z, 4 * a + e, 4 * b, 4), t(XK, C * e, C * e + C), t("tt18", a // 16, b // 16), t(XC, C * e + a, C * e + b), A.add)
+                if i == 0 and e == 0:
+                    cp(t("tt18", 9, 18), f("hi", 0, 9))
             n = max(128, b - a)
             p = 0 if i == 0 else C1 + 128 * (i - 1)
             q, s = t(zq, p, p + n), t(zs, p, p + n)
@@ -499,28 +463,19 @@ def rank_program(g, core, T, topo):
         n = send(dst, "ha%d" % r, t(lq, 0, C1), t(hq, 0, C1), [t(hq, 0, C1)], True)
         n += send(dst, "ha%d" % r, t(ls, 0, C1), t(hs, 0, C1), [t(hs, 0, C1)])
         if r == 0:
-            constants3()
-        tt(f("x8", 1, 216, 3), (low[0], low[1], low[1] + 72, 1), f("JM8", 0, 72), A.is_equal)
-        gop(f("x8", 0, 240, 3), low, t("oR", 0, 5), f("JM8"), A.is_equal)
+            ts(t("ki", 0, 18), t("kli"), 15, A.bitwise_and)
+            ts(t("ki", 18, 36), t("kli"), 4, A.arith_shift_right)
+            ts(t("ki", 0, 18), t("ki", 0, 18), 18, A.mult)
         quant(t(hq, C1, C1 + 128), t(hs, C1, C1 + 128), t(H, 4 * (E - 128), 4 * E))
         m = send(dst, "hb%d" % r, t(lq, C1, E), t(hq, C1 + 128 - C2, C1 + 128), [t(hq, C1, C1 + 128)], True)
         m += send(dst, "hb%d" % r, t(ls, C1, E), t(hs, C1 + 128 - C2, C1 + 128), [t(hs, C1, C1 + 128)])
         arrives("ha%d" % r, n, [t(lq, 0, C1), t(ls, 0, C1)])
         arrives("hb%d" % r, m, [t(lq, C1, E), t(ls, C1, E)])
-        scan(f("xs8"), f("z8"), f("x8", 0, 216), A.mult, A.add)
-        layer(2, E, C, 12)
         if r == 0:
-            constants4()
-        tt(f("up", 0, 9), f("cc18", 0, 9), f("xs8", 23, 216, 24), A.subtract)
-        cp(t("tt18", 0, 9), f("xs8", 23, 216, 24))
-        cp(t("tt18", 9, 18), f("up", 0, 9))
-        if r == 0:
-            ts(t("ki", 0, 18), t("kli"), 15, A.bitwise_and)
-            ts(t("ki", 18, 36), t("kli"), 4, A.arith_shift_right)
-            ts(t("ki", 0, 18), t("ki", 0, 18), 18, A.mult)
             tt(t("ki", 36, 54), t("ki", 0, 18), t("ki", 18, 36), A.add)
             cp(t("ks"), t("ki", 36, 54))
-            gop(t(kk), t(kf), t("ks"), f("m144"), A.add)
+            ts(t(kk), t(kf), -144.0, A.add, off=t("ks"))
+        layer(2, E, C, 12)
         gop(f("n16w"), t(kk), t("tt18"), f("M16n"), A.add)
         actg(t(nf), t(kk), t("tt18"), 1.0, 144.0)
         scan(f("n16s"), f("d16b"), f("n16w"), A.min, A.max)

@@ -10,23 +10,23 @@ F4 = "float8_e4m3fn_x4"
 SEG = 18
 
 SCRATCH = {
-    "ub": ("sbuf", [128, 512], "bfloat16"), "vb": ("sbuf", [128, 512], "bfloat16"), "et": ("sbuf", [128, 2048], "bfloat16"),
-    "one": ("sbuf", [128, 512], "bfloat16"),
+    "ub": ("sbuf", [128, 512], "bfloat16"), "vb": ("sbuf", [128, 512], "bfloat16"), "et": ("sbuf", [128, 516], "bfloat16"),
+    "one": ("sbuf", [128, 516], "bfloat16"),
     "uq": ("sbuf", [128, 128], F4), "us": ("sbuf", [128, 128], "uint8"),
     "ur": ("sbuf", [128, 128], F4), "urs": ("sbuf", [128, 128], "uint8"),
     "vq": ("sbuf", [128, 128], F4), "vs": ("sbuf", [128, 128], "uint8"),
     "eq": ("sbuf", [128, 512], F4), "es": ("sbuf", [128, 512], "uint8"),
     "wq": ("sbuf", [128, 512], F4), "wp": ("sbuf", [128, 512], "uint8"),
     "kli": ("sbuf", [128, 18], "int32"), "ki": ("sbuf", [128, 54], "int32"),
-    "kld": ("dram", [128, 18], "int32"), "lk0": ("dram", [128, 18], "int32"),
+    "klf": ("sbuf", [128, 18], "float32"), "kld": ("dram", [128, 18], "float32"), "lk0": ("dram", [128, 18], "float32"),
     "nd1": ("dram", [128, 18], "float32"), "nd2": ("dram", [128, 18], "float32"),
     "lk1": ("dram", [128, 18], "float32"), "lk2": ("dram", [128, 18], "float32"),
-    "kf0": ("sbuf", [128, C], "int32"), "kf1": ("sbuf", [128, C], "float32"), "kf2": ("sbuf", [128, C], "float32"),
+    "kf0": ("sbuf", [128, C], "float32"), "kf1": ("sbuf", [128, C], "float32"), "kf2": ("sbuf", [128, C], "float32"),
     "pI": ("sbuf", [128, 8], "int32"), "uI": ("sbuf", [128, 24], "int32"), "pF": ("sbuf", [128, 24], "float32"),
     "cI": ("sbuf", [128, 48], "int32"),
     "uo": ("sbuf", [128, 24], "uint16"), "ks": ("sbuf", [128, 18], "uint16"),
-    "oC": ("sbuf", [128, 16], "uint16"), "oI": ("sbuf", [128, 16], "uint16"),
-    "oA": ("sbuf", [128, 6], "uint16"), "oE": ("sbuf", [128, 4], "uint16"),
+    "oC": ("sbuf", [128, 28], "uint16"), "oI": ("sbuf", [128, 28], "uint16"),
+    "oD": ("sbuf", [128, 12], "uint16"), "oK": ("sbuf", [128, 24], "uint16"), "oA": ("sbuf", [128, 6], "uint16"), "oE": ("sbuf", [128, 4], "uint16"),
     "oT0": ("sbuf", [128, 10], "uint16"), "oT1": ("sbuf", [128, 6], "uint16"), "oT2": ("sbuf", [128, 6], "uint16"), "oT3": ("sbuf", [128, 6], "uint16"),
     "tt18": ("sbuf", [128, 18], "uint16"),
     "ps": ("psum", [128, 4096], "float32"),
@@ -40,8 +40,10 @@ for _i in range(4):
 for _i in range(3):
     SCRATCH["XK%d" % _i] = ("sbuf", [128, 4 * C], "bfloat16")
     SCRATCH["XC%d" % _i] = ("sbuf", [128, 4 * C], "bfloat16")
+    SCRATCH["ZG%d" % _i] = ("sbuf", [128, 2 * C], "bfloat16")
+    SCRATCH["BG%d" % _i] = ("sbuf", [128, 2 * C], "bfloat16")
     SCRATCH["Z%d" % _i] = ("sbuf", [128, 4 * C], "bfloat16")
-    SCRATCH["H%d" % _i] = ("sbuf", [128, 4 * E], "bfloat16")
+    SCRATCH["H%d" % _i] = ("sbuf", [128, 4 * (C1 + 128)], "bfloat16")
     SCRATCH["B%d" % _i] = ("sbuf", [128, 4 * C], "bfloat16")
     SCRATCH["zq%d" % _i] = ("sbuf", [128, C1 + 256], F4)
     SCRATCH["zs%d" % _i] = ("sbuf", [128, C1 + 256], "uint8")
@@ -53,19 +55,18 @@ for _i in range(3):
     SCRATCH["nf%d" % _i] = ("sbuf", [128, C], "float32")
     SCRATCH["kk%d" % _i] = ("sbuf", [128, C], "float32")
 _ROWS = {
-    "t16": 288, "t32": 32, "M16n": 288, "tmp": 288, "pos": 16, "xx": 16, "hb": 96, "hz": 96, "hs": 96, "ww": 16, "t1": 16, "bb": 16,
-    "cf": 16, "a1": 16, "a2": 16, "up": 16, "mem": 32, "rk": 32, "c2": 16, "cb": 16, "cu": 16, "su": 16, "en": 16, "hi": 16, "t8": 80, "e8": 80,
-    "JA": 72, "JB": 144,
+    "t16": 288, "t32": 32, "M16n": 288, "tmp": 288, "pos": 16, "bb": 16, "bo": 16, "a1": 16, "a2": 16, "mem": 32, "rk": 32,
+    "cb": 16, "cu": 16, "su": 16, "en": 16, "hi": 16, "t8": 80, "e8": 80, "JA": 72, "JB": 144, "M144": 176,
 }
 _ROWS2 = {
-    "sg": 288, "fx": 144, "sw": 32, "val": 256, "K": 256, "lk": 192, "lz": 208, "ls": 192, "ek": 64, "ez": 64, "es": 64,
-    "bc": 160, "BT": 160, "M": 288, "MS": 288, "M8": 144,
-    "sf": 288, "wv": 288, "Fa": 160, "Fb": 160, "Fc": 160, "RD": 128, "La": 160, "Lb": 160, "Lc": 160, "Ld": 160,
+    "sg": 288, "fx": 144, "sw": 32, "val": 448, "K": 448, "lk": 176, "uk": 176, "lz": 192, "ls": 192, "ue": 176, "ek": 64, "ez": 64, "es": 64,
+    "BT": 320, "M": 288, "MS": 288, "M8": 144,
+    "sf": 288, "wv": 288, "Fa": 160, "Fb": 160, "Fc": 160, "Fd": 160, "RD": 128, "La": 160, "Lb": 160, "Lc": 160, "Ld": 160,
     "ts": 160, "rs": 128, "fc": 288, "fj": 144, "J": 80, "x": 288, "z": 288, "xs": 288,
-    "n16w": 288, "n16s": 288, "d16b": 288,
+    "n16w": 288, "n16s": 288, "d16b": 288, "klw": 176, "kls": 176,
 }
-_ROW_OF = {"F1": "Fa", "F2": "Fb", "F3": "Fc", "F4": "Fa", "F7": "Fb", "F10": "Fc", "F17": "Fa", "L2": "La", "L3": "Lb", "L4": "Lc",
-           "L7": "La", "L10": "Ld", "L17": "Lc", "L24": "Lb", "L41": "Ld", "L58": "La", "L75": "Lb"}
+_ROW_OF = {"F1": "Fa", "F2": "Fb", "F3": "Fc", "F4": "Fd", "F5": "Fa", "F9": "Fb", "F13": "Fc", "F22": "Fd",
+           "L4": "La", "L6": "Lb", "L10": "Lc", "C10": "La", "L19": "Lb", "L28": "Ld", "C28": "La", "L50": "Lb", "L72": "Lc"}
 OFF = {}
 for _b, _t, _d in (("F", _ROWS, "float32"), ("G", _ROWS2, "bfloat16")):
     _n = 0
@@ -225,105 +226,107 @@ def rank_program(g, core, T, topo):
     dma("s", "dk", T.kli[:, :], T.kl[:, :], [], [t("kli")])
     dma("s", "du", T.ub[:, :], T.u[:, :], [], [t("ub")])
     dma("y", "dx1", T.X0[:, 640:1152], T.x[:, 640:1152], [], [t("X0", 640, 1152)])
-    dma("y", "dkl", T.kld[:, :], T.kl[:, :], [], [t("kld")])
-    need("y", "dx1", 16)
-    dma("y", "dw", T.wq[:, 0:512].bitcast(dt.uint8), T.wc[:, :], [], [t("wq")])
-    dma("y", "dw", T.wp[:, 0:512], T.ws[:, :], [], [t("wp")])
-    dma("y", "dv", T.vb[:, :], T.v[:, :], [], [t("vb")])
 
     iota(t("pI", 0, 1), [[0, 1]], 0, 1)
-    iota(t("uI", 0, 12), [[16, 12]])
-    iota(f("bb", 12, 16), [[-1, 4]], 3)
-    iota(t("uI", 12, 22), [[SEG, 5], [0, 2]], 6 * SEG - 1)
-    iota(f("up", 12, 16), [[0, 4]], 1)
+    iota(t("uI", 0, 10), [[16, 10]])
     iota(f("t32"), [[1, 32]])
-    for k in range(4):
-        iota(f("rk", 16 >> k, 32 >> k), [[0, 16 >> k]], 8 >> k)
+    iota(f("bb", 0, 9), [[-1, 9]], 8)
+    iota(f("bo", 0, 10), [[0, 5], [16, 2]])
     iota(f("wv", 128, 288, 2), [[-64, 5], [-2, 16]], 286)
     iota(f("sw", 0, 32, 16), [[-2, 2]], 1)
     iota(f("wv", 0, 144, 2), [[4, 72]])
     iota(f("t16"), [[0, 18], [1, 16]])
     iota(f("fx"), [[0, 144]], -1)
-    iota(f("lz", 0, 11 * SEG), [[0, 11], [512, SEG]])
+    iota(f("lz"), [[0, 6], [512, 32]])
+    iota(f("lz", 32, 33), [[0, 1]], 512)
+    iota(f("ls", 176, 192), [[0, 16]])
     iota(f("t8"), [[0, 10], [1, 8]])
     iota(f("ez"), [[0, 4], [512, 16]])
     iota(f("J"), [[2, 80]])
-    partner = [T.cores[rank ^ m] for m in MASKS]
-    arrives("lr0", send(partner[0], "lr0", t("lk0"), t("kld"), [t("kld")]), [t("lk0")])
-    iota(f("JB"), [[256, 9], [17, 16]])
-    iota(f("JA"), [[256, 9], [33, 8]])
-    for a, step, c in ((0, 4, 1), (1, 4, -1), (2, 4, -1), (3, 4, 1), (0, 32, 0)):
-        iota(f("z", a, 288, step), [[0, 288 // step]], c)
     iota(f("x", 3, 288, 4), [[0, 72]])
-    iota(f("d16b"), [[0, 18], [16384, 16]], -8192)
+    iota(f("z", 3, 288, 4), [[0, 72]], 1)
+    partner = [T.cores[rank ^ m] for m in MASKS]
 
     def pcol(i):
         return t("pF", i, i + 1)
 
     fill(("G", OFF["sf"][1] + 1, OFF["ts"][1], 2), 0.0)
-    fill(f("hz"), 2.0)
     ts(t("pI", 1, 2), t("pI", 0, 1), 15, A.bitwise_and)
     ts(t("pI", 2, 3), t("pI", 0, 1), 16, A.bitwise_and)
     ts(t("pI", 3, 4), t("pI", 0, 1), 14, A.bitwise_and)
     ts(t("pI", 4, 5), t("pI", 0, 1), 1, A.bitwise_and)
-    fill(f("hz", 0, 96, 6), 0.0)
+    for a, b, c in ((0, 1, 2.0), (1, 2, 4.0), (2, 4, 8.0), (4, 8, 16.0), (8, 16, 32.0), (16, 32, 64.0)):
+        fill(f("rk", a, b), c)
     cp(t("pF", 1, 5), t("pI", 1, 5))
     P16, ODD16, P14, PAR = [pcol(i) for i in range(1, 5)]
-    cp(t("uo", 0, 22), t("uI", 0, 22))
-    ts(f("pos", 0, 12), t("uI", 0, 12), P16, A.add)
-    actf(pcol(5), P16, IDENT, -0.125, 3.875)
-    actf(pcol(6), P16, IDENT, 1.0, 2.0)
+    for a, b, step, c in ((0, 12, 1, 2), (2, 3, 1, 4), (12, 24, 1, 284), (14, 15, 1, 282)):
+        fill(t("oC", a, b, step), c)
+    cp(t("uo", 0, 10), t("uI", 0, 10))
+    ts(f("mem", 0, 16), f("t32", 0, 16), P16, A.is_equal)
+    ts(f("pos", 0, 10), t("uI", 0, 10), P16, A.add)
+    actf(pcol(5), P16, IDENT, -1.0 / 64, 31.0 / 64)
+    actf(pcol(6), ODD16, IDENT, 11.0, 0.0)
     actf(pcol(9), P14, IDENT, 0.5, 0.0)
-    actf(f("xx", 12, 16), f("bb", 12, 16), IDENT, 0.0, pcol(6))
     actf(pcol(14), PAR, IDENT, -2.0, 1.0)
     actf(f("cb", 0, 9), f("pos", 0, 9), IDENT, 2.0, -147.5)
     actf(f("cu", 0, 9), f("pos", 0, 9), IDENT, 4.0, -143.0)
     actf(pcol(15), pcol(14), IDENT, -4.0, 0.5)
-    ts(t("cI", 16, 28), f("pos", 0, 12), 1.0 / SEG, A.mult, -0.47, A.add)
-    ts(f("a1", 0, 12), t("cI", 16, 28), float(-SEG), A.mult)
-    ts(f("a2", 0, 12), t("cI", 16, 28), 5.0, A.is_ge, 5.0, A.mult)
-    ts(f("bb", 0, 12), t("cI", 16, 28), -1.0, A.mult, 8.0, A.add)
-    tt(f("xx", 0, 12), f("a1", 0, 12), f("pos", 0, 12), A.add)
-    ts(f("up", 0, 12), t("cI", 16, 28), 5.0, A.is_lt)
-    tt(f("bb", 0, 12), f("bb", 0, 12), f("a2", 0, 12), A.add)
-    for k, th in enumerate((10.0, 6.0, 4.0, 3.0, 2.0, 1.0)):
-        ts(f("hb", k, 96, 6), f("xx"), th, A.is_ge)
-    ts(f("t1"), f("xx"), -2.0, A.add, 0.0, A.max)
-    ts(t("ki", 2, 32), f("rk", 2, 32), pcol(5), A.mult, -0.47, A.add)
-    scan(f("hs"), f("hz"), f("hb"), A.mult, A.add)
-    tt(f("bb"), f("bb"), f("hb", 3, 96, 6), A.subtract)
+    fill(t("oI"), 0)
+    tt(f("a1"), f("mem", 0, 16), f("rk", 0, 16), A.mult)
+    ts(f("a2", 0, 9), f("bb", 0, 9), f("mem", 0, 1), A.add, -1.0, A.add)
+    fill(t("oI", 4, 7, 2), 16)
+    run("v", lambda: g.vector.tensor_reduce(ap(pcol(7)), ap(f("a1")), AxisListType.X, A.add), [f("a1")], [pcol(7)])
+    fill(t("oI", 16, 19, 2), 16)
+    ts(t("ki", 2, 32), f("rk", 2, 32), pcol(5), A.mult, -0.49, A.add)
+    ts(f("a2", 0, 9), f("a2", 0, 9), pcol(7), A.mult, 0.25, A.mult)
+    for a, b, step, c in ((1, 10, 2, 0), (13, 22, 2, 0), (24, 28, 1, 5)):
+        ts(t("oI", a, b, step), f("bo", c, c + len(range(a, b, step))), f("mem", 0, 1), A.mult, P16, A.add)
+    ts(f("a2", 0, 9), f("a2", 0, 9), P16, A.add, -0.25, A.add)
     tt(f("mem", 2, 32), t("ki", 2, 32), f("t32", 2, 32), A.is_equal)
-    ts(f("ww"), f("hs", 5, 96, 6), 1.0, A.add, 0.125, A.mult)
-    ts(t("k4t0", 20, 38), t("kli"), 4, A.mult, 1, A.add)
-    tt(f("sw", 1, 16), f("mem", 2, 32, 2), f("mem", 3, 32, 2), A.subtract)
-    tt(f("cf"), f("ww"), f("bb"), A.mult)
-    ts(t("k4t0", 40, 58), t("kli"), 4, A.mult, 2, A.add)
-    tt(f("cf"), f("cf"), f("t1"), A.add)
-    ts(t("k4t0", 60, 78), t("kli"), 4, A.mult, 3, A.add)
-    ts(t("cI", 0, 16), f("cf"), -0.44, A.add)
-    ts(t("cI", 32, 48), f("cf"), 2.0, A.mult, -0.44, A.add)
+    cp(t("cI", 0, 9), f("a2", 0, 9))
     ts(t("k4t0", 0, 18), t("kli"), 4, A.mult, 0, A.add)
+    tt(f("sw", 1, 16), f("mem", 2, 32, 2), f("mem", 3, 32, 2), A.subtract)
+    ts(t("oC", 1, 10, 2), t("cI", 0, 5), 2.0, A.mult)
+    ts(t("oC", 13, 22, 2), t("cI", 0, 5), -2.0, A.mult, 286.0, A.add)
+    ts(t("oC", 24, 28), t("cI", 5, 9), -2.0, A.mult, 286.0, A.add)
+    for e in range(1, 4):
+        ts(t("k4t0", 20 * e, 20 * e + 18), t("kli"), 4, A.mult, e, A.add)
     cp(t("kt0"), t("kli"))
+    cp(t("klf"), t("kli"))
+    dma("y", "dkl", T.kld[:, :], T.klf[:, :], [t("klf")], [t("kld")])
+    need("y", "dx1", 16)
+    dma("y", "dw", T.wq[:, 0:512].bitcast(dt.uint8), T.wc[:, :], [], [t("wq")])
+    dma("y", "dw", T.wp[:, 0:512], T.ws[:, :], [], [t("wp")])
+    for a, step, c in ((0, 4, 1), (1, 4, -1), (2, 4, -1), (0, 32, 0)):
+        iota(f("z", a, 288, step), [[0, 288 // step]], c)
+    arrives("lr0", send(partner[0], "lr0", t("lk0"), t("kld"), [t("kld")]), [t("lk0")])
+    iota(f("JB"), [[256, 9], [17, 16]])
+    iota(f("JA"), [[256, 9], [33, 8]])
+    iota(f("d16b"), [[0, 18], [16384, 16]], -8192)
+    equal(f("M16n", 0, 160), f("t16", 0, 160), P16, f("tmp", 0, 160))
+
+    def weights(a, b, q):
+        if q == "s":
+            actg(f("val", 16 * a, 16 * b), f("wv"), t("oC", a, b))
+        else:
+            gop(f("K", 16 * a, 16 * b), f("sw", 0, 17), t("oI", a, b), f("val", 16 * a, 16 * b), A.mult)
+
+    weights(0, 11, "s")
     quant(t("uq"), t("us"), t("ub"))
-    ts(f("a1"), t("cI", 0, 16), -4.0, A.mult, 286.0, A.add)
-    ts(f("a2"), t("cI", 0, 16), 2.0, A.mult)
     run("v", lambda: g.vector.tensor_copy(T.ur[:, 0:128].bitcast(dt.uint32), T.uq[:, 0:128].bitcast(dt.uint32).indirect(T.uo[:, 0:8])),
         [t("uq"), t("uo")], [t("ur")])
-    equal(f("M16n"), f("t16"), P16, f("tmp"))
     run("s", lambda: g.scalar.activation(T.urs[:, 0:128], T.us[:, 0:128].indirect(T.uo[:, 0:8]), COPY), [t("us"), t("uo")], [t("urs")])
-    tt(f("a1"), f("a1"), f("up"), A.mult)
-    tt(f("c2"), t("cI", 32, 48), f("a2"), A.subtract)
-    tt(f("a1"), f("a1"), f("a2"), A.add)
-    ts(f("c2"), f("c2"), 16.0, A.mult)
-    cp(t("oC"), f("a1"))
-    tt(f("c2"), f("c2"), f("t1"), A.add)
-    actg(f("val"), f("wv"), t("oC"))
+    weights(12, 23, "s")
+    weights(0, 11, "v")
     act(f("M", 0, 288, 2), f("M16n", 0, 144), 256.0)
     act(f("M", 1, 288, 2), f("M16n", 1, 145), -4096.0)
-    equal(f("e8"), f("t8"), pcol(9), f("tmp", 0, 80))
-    act(f("MS"), f("M"), 1.0 / 64)
-    act(f("M8", 0, 144, 2), f("e8", 0, 72), 4.0)
-    act(f("M8", 1, 144, 2), f("e8", 1, 73), -64.0)
+    weights(24, 28, "s")
+
+    def picks():
+        equal(f("e8"), f("t8"), pcol(9), f("tmp", 0, 80))
+        act(f("MS"), f("M"), 1.0 / 64)
+        act(f("M8", 0, 144, 2), f("e8", 0, 72), 4.0)
+        act(f("M8", 1, 144, 2), f("e8", 1, 73), -64.0)
 
     def state(r, h):
         a, b = HS[h]
@@ -334,16 +337,16 @@ def rank_program(g, core, T, topo):
         mm(bank(2 + h, b - a), t("ur"), t("urs"), t("xq%d" % r, a, b), t("xs%d" % r, a, b))
 
     state(0, 0)
-    cp(t("oI"), f("c2"))
     state(0, 1)
     scores(0, 0)
     scores(0, 1)
     fill(f("fx", 143, 144), 0.5)
-    gop(f("K"), f("sw", 0, 17), t("oI"), f("val"), A.mult)
-    run("q", lambda: g.iota(T.one[:, 0:512], [[0, 512]], 1, 0, allow_small_or_imprecise_dtypes=True), [], [t("one")])
-    for e in range(4):
-        run("q", lambda: g.affine_select(T.et[:, 512 * e:512 * e + 512], T.one[:, 0:512], [[-1, 512]], A.is_equal, 0.0, e, 4),
-            [t("one")], [t("et", 512 * e, 512 * e + 512)])
+    weights(12, 23, "v")
+    run("q", lambda: g.iota(T.one[:, 0:516], [[0, 516]], 1, 0, allow_small_or_imprecise_dtypes=True), [], [t("one")])
+    run("q", lambda: g.affine_select(T.et[:, 0:516], T.one[:, 0:516], [[-1, 516]], A.is_equal, 0.0, 3, 4), [t("one")], [t("et")])
+
+    def unit(b):
+        quant(t("eq", 128 * b, 128 * b + 128), t("es", 128 * b, 128 * b + 128), t("et", 3 - b, 515 - b))
 
     def marks():
         actf(pcol(10), P16, IDENT, -1.0 / 16, pcol(14))
@@ -354,8 +357,13 @@ def rank_program(g, core, T, topo):
         actf(pcol(10), pcol(10), IDENT, 1.0, -1.0)
         actf(f("JA", 0, 1), f("JA", 0, 1), IDENT, 1.0, pcol(12))
         actf(f("JB"), f("JB"), IDENT, 1.0 / 16, pcol(10))
-        actf(f("M16n"), f("M16n"), IDENT, 4096.0, -4096.0)
+        actf(f("M16n", 160, 288), f("M16n", 0, 128), IDENT, 4096.0, -4096.0)
+        actf(f("M16n", 0, 160), f("M16n", 0, 160), IDENT, 4096.0, -4096.0)
+        actf(f("M144"), f("M16n", 0, 176), IDENT, 1.0, -144.0)
         actf(f("JB", 0, 1), f("JB", 0, 1), IDENT, 1.0, pcol(12))
+
+    def above(a, b, c, r):
+        ts(t("oK", a, b, 2), f("pos", 0, (b - a + 1) // 2), 0.0, A.mult, t("nf%d" % r, c, c + 1), A.add)
 
     def even(n):
         return f(n, 0, 160, 2)
@@ -370,7 +378,7 @@ def rank_program(g, core, T, topo):
     for r in range(3):
         X, XK, XC, Z, H, B, kt = ["%s%d" % (n, r) for n in ("X", "XK", "XC", "Z", "H", "B", "kt")]
         zq, zs, hq, hs, lq, ls, nf, kk = ["%s%d" % (n, r) for n in ("zq", "zs", "hq", "hs", "lq", "ls", "nf", "kk")]
-        kf, lk = "kf%d" % r, "lk%d" % r
+        kf, lk, ZG, BG = "kf%d" % r, "lk%d" % r, "ZG%d" % r, "BG%d" % r
 
         def xk(e):
             actg(t(XK, C * e, C * e + C), t(X), t("k4t%d" % r, 20 * e, 20 * e + 18), 0.5)
@@ -382,71 +390,114 @@ def rank_program(g, core, T, topo):
         xk(1)
         for h in range(2):
             ts(f("sg", HS[h][0], HS[h][1]), bank(2 + h, HS[h][1] - HS[h][0]), 0.0, A.is_gt, -0.5, A.add)
+            if r and h == 0:
+                for a, b, c in ((4, 11, 1), (12, 13, 142), (14, 15, 141)):
+                    above(a, b, c, r - 1)
         if r:
             xk(2)
-        gop(f("sf", 0, 288, 2), f("sg"), t(kt, 0, 9), f("fx"), A.max)
-        gop(f("lk"), f("sf"), t("oC", 0, 12), f("K", 0, 192), A.mult)
-        scan(f("ls"), f("lz", 0, 192), f("lk"), A.min, A.max)
-        gop(f("ek"), f("sf"), t("oC", 12, 16), f("K", 192, 256), A.mult)
-        actg(f("bc"), f("ls"), t("uo", 12, 22))
+        else:
+            picks()
+        def bits():
+            gop(f("sf", 0, 288, 2), f("sg"), t(kt, 0, 9), f("fx"), A.max)
+
+        if r == 0:
+            bits()
+        win, off = ("sg", "oK") if r else ("sf", "oC")
+        gop(f("lk"), f(win), t(off, 0, 11), f("K", 0, 176), A.mult)
+        gop(f("uk"), f(win), t(off, 12, 23), f("K", 192, 368), A.mult)
+        scan(f("ls", 0, 176), f("lz", 16, 192), f("lk"), A.min, A.max)
+        scan(f("ue"), f("lz", 16, 192), f("uk"), A.min, A.max)
         xk(3 if r else 2)
-        ts(t("oA", 0, 5), f("ls", SEG - 1, 5 * SEG, SEG), ODD16, A.add)
-        scan(f("es"), f("ez"), f("ek"), A.min, A.max)
-        scan(f("fc"), f("sf"), f("MS"), A.max, A.add, -64.0)
-        ts(t("oE"), f("es", 15, 64, 16), ODD16, A.add)
-        run("v", lambda: g.vector.transpose(ap(f("BT")), ap(f("bc"))), [f("bc")], [f("BT")])
-        scan(f("fj"), f("sf", 0, 144), f("M8"), A.max, A.add, -64.0)
+        for a, b in ((0, 32), (160, 16)):
+            run("v", lambda: g.vector.transpose(ap(f("BT", a, a + 160)), ap(f("ls", b, b + 160))), [f("ls", b, b + 160)], [f("BT", a, a + 160)])
+        ts(t("oA", 0, 5), f("ue", 32, 176, 32), pcol(6), A.add)
         gat(even("F1"), f("BT"), t("oA", 0, 5))
-        gop(even("L2"), f("BT"), t("oA", 0, 5), f("J"), A.min)
         end = table(0, "F1")
-        ts(f("su", 0, 9), f("fc", 30, 288, 32), -4.0, A.add, 2.0, A.mult)
+        tt(even("L4"), even("F1"), f("J"), A.min)
         end()
-        actg(f("RD", 0, 128, 2), f("BT"), t("oE"))
         if r == 0:
             xk(3)
+            weights(24, 28, "v")
         for i in range(16):
             dma("y", "df%d" % r, T[kf][i:128:16, :], T[lk][:, :], [t(lk)], [(kf, i, C, 16)])
-        actg(even("F2"), f("F1"), t("oT0", 0, 5))
-        actg(even("F3"), f("F2"), t("oT0", 0, 5))
-        lowest("L3", "L2", 0, f("J"))
+        if r == 1:
+            dma("y", "dv", T.vb[:, :], T.v[:, :], [], [t("vb")])
+        for a, b in (("F2", "F1"), ("F3", "F2"), ("F4", "F3"), ("F5", "F4")):
+            if r == 0 and a == "F2":
+                gat(even(a), f(b), t("oT0", 0, 5))
+            else:
+                actg(even(a), f(b), t("oT0", 0, 5))
+        if r:
+            bits()
+        tt(even("L4"), even("L4"), even("F2"), A.min)
+        gop(f("ek"), f("sf"), t("oC", 24, 28), f("K", 384, 448), A.mult)
+        scan(f("fc"), f("sf"), f("MS"), A.max, A.add, -64.0)
+        scan(f("es"), f("ez"), f("ek"), A.min, A.max)
+        tt(even("L4"), even("L4"), even("F3"), A.min)
+        ts(t("oE"), f("es", 15, 64, 16), pcol(6), A.add)
+        end = table(1, "F4")
+        tt(even("L6"), even("L4"), even("F4"), A.min)
+        end()
+        scan(f("fj"), f("sf", 0, 144), f("M8"), A.max, A.add, -64.0)
+        tt(even("L6"), even("L6"), even("F5"), A.min)
+        actg(even("F9"), f("F5"), t("oT1", 0, 5))
+        actg(even("F13"), f("F9"), t("oT1", 0, 5))
         tt(f("x", 31, 288, 32), f("fc", 30, 288, 32), f("cb", 0, 9), A.add)
-        lowest("L4", "L3", 0, f("J"))
-        scan(f("rs"), f("RD"), f("M", 0, 128), A.max, A.add, -4096.0)
-        end = table(1, "F3")
-        actg(even("F4"), f("F3"), t("oT0", 0, 5))
+        lowest("L10", "L6", 1, "L4")
+        end = table(2, "F9")
+        cp(even("C10"), even("L10"))
+        end()
+        if r:
+            ts(f("su", 0, 9), f("fc", 30, 288, 32), -4.0, A.add, 2.0, A.mult)
+        actg(even("F22"), f("F13"), t("oT2", 0, 5))
+        actg(f("RD", 0, 128, 2), f("BT"), t("oE"))
+        if r == 0:
+            ts(t("ki", 0, 18), t("kli"), 15, A.bitwise_and)
+            ts(t("ki", 18, 36), t("kli"), 4, A.arith_shift_right)
+            ts(t("ki", 0, 18), t("ki", 0, 18), 18, A.mult)
+        lowest("L19", "L10", 2, "C10")
+        if r == 0:
+            ts(f("su", 0, 9), f("fc", 30, 288, 32), -4.0, A.add, 2.0, A.mult)
         ts(f("en", 0, 9), f("fj", 14, 144, 16), pcol(14), A.mult, pcol(15), A.add)
+        end = table(3, "F22")
+        lowest("L28", "L19", 2, "L10")
         end()
-        actg(even("F7"), f("F4"), t("oT1", 0, 5))
-        tt(f("z", 31, 288, 32), f("su", 0, 9), f("en", 0, 9), A.mult)
-        lowest("L7", "L4", 1, "L3")
-        end = table(2, "F7")
-        actg(even("F10"), f("F7"), t("oT1", 0, 5))
-        lowest("L10", "L7", 1, "L3")
-        end()
-        actg(even("F17"), f("F10"), t("oT2", 0, 5))
-        lowest("L17", "L10", 2, "L7")
-        end = table(3, "F17")
-        lowest("L24", "L17", 2, "L7")
-        end()
+        cp(even("C28"), even("L28"))
+        actf(t(H, 4 * E, 4 * C1 + 512), f("t16", 0, 4 * (C1 + 128 - E)), IDENT, 0.0, 0.0)
         if r == 0:
             marks()
         else:
             actg(t(kk), t(kf), t(kt), 1.0, -144.0)
+        scan(f("rs"), f("RD"), f("M", 0, 128), A.max, A.add, -4096.0)
+        lowest("L50", "L28", 3, "C28")
         ts(t("oT0", 5, 9), f("rs", 30, 128, 32), -256.0, A.add)
-        lowest("L41", "L24", 3, "L17")
-        lowest("L58", "L41", 3, "L17")
-        lowest("L75", "L58", 3, "L17")
-        gop(f("x", 0, 288, 2), f("L75"), t("oT0", 0, 9), f("JB"), A.is_equal)
-        tt(f("x", 1, 288, 4), f("L75", 0, 144, 2), f("JA", 0, 72), A.is_equal)
+        lowest("L72", "L50", 3, "L28")
+        tt(f("z", 31, 288, 32), f("su", 0, 9), f("en", 0, 9), A.mult)
+        gop(f("x", 0, 288, 2), f("L72"), t("oT0", 0, 9), f("JB"), A.is_equal)
+        tt(f("x", 1, 288, 4), f("L72", 0, 144, 2), f("JA", 0, 72), A.is_equal)
+        if r == 0:
+            tt(t("ki", 36, 54), t("ki", 0, 18), t("ki", 18, 36), A.add)
         scan(f("xs"), f("z"), f("x"), A.mult, A.add)
+        if r == 0:
+            cp(t("ks"), t("ki", 36, 54))
         ts(t("tt18", 0, 9), f("xs", 31, 288, 32), 144.0, A.add)
         tt(f("hi", 0, 9), f("cu", 0, 9), f("xs", 31, 288, 32), A.subtract)
 
+        def pair(e, a, b):
+            if e >= 2:
+                tt(t(Z, 4 * a + e, 4 * b, 4), t(ZG, C * (e - 2) + a, C * (e - 2) + b), t(XC, C * e + a, C * e + b), A.add)
+            else:
+                gop(t(Z, 4 * a + e, 4 * b, 4), t(XK, C * e, C * e + C), t("tt18", a // 16, b // 16), t(XC, C * e + a, C * e + b), A.add)
+
         def layer(i, a, b, at):
             for e in range(4):
-                gop(t(Z, 4 * a + e, 4 * b, 4), t(XK, C * e, C * e + C), t("tt18", a // 16, b // 16), t(XC, C * e + a, C * e + b), A.add)
+                if (i, e) != (2, 0) or r == 0:
+                    pair(e, a, b)
                 if i == 0 and e == 0:
                     cp(t("tt18", 9, 18), f("hi", 0, 9))
+                    for a2, b2 in ((0, C1), (C1, E)):
+                        for e2 in (2, 3):
+                            actg(t(ZG, C * (e2 - 2) + a2, C * (e2 - 2) + b2), t(XK, C * e2, C * e2 + C), t("tt18", a2 // 16, b2 // 16))
             n = max(128, b - a)
             p = 0 if i == 0 else C1 + 128 * (i - 1)
             q, s = t(zq, p, p + n), t(zs, p, p + n)
@@ -454,35 +505,47 @@ def rank_program(g, core, T, topo):
             for k in range(4):
                 mm(bank(at + k, n), t("wq", 128 * k, 128 * k + 128), t("wp", 128 * k, 128 * k + 128), q, s)
                 o, c = bank(at + k, n), t(B, C * k + a, C * k + b) if i == 2 else t(H, 4 * a + k, 4 * b, 4)
-                act(c, (o[0], o[2] - (b - a), o[2], 1), 0.03125)
+                o = (o[0], o[2] - (b - a), o[2], 1)
+                if i == 1 and k % 2:
+                    later.append((c, o))
+                else:
+                    act(c, o, 0.03125)
 
+        later = []
         layer(0, 0, C1, 4)
         layer(1, C1, E, 8)
         quant(t(hq, 0, C1), t(hs, 0, C1), t(H, 0, 4 * C1))
         dst = partner[r]
         n = send(dst, "ha%d" % r, t(lq, 0, C1), t(hq, 0, C1), [t(hq, 0, C1)], True)
-        n += send(dst, "ha%d" % r, t(ls, 0, C1), t(hs, 0, C1), [t(hs, 0, C1)])
+        for e in (2, 3):
+            actg(t(ZG, C * (e - 2) + E, C * (e - 2) + C), t(XK, C * e, C * e + C), t("tt18", E // 16, C // 16))
         if r == 0:
-            ts(t("ki", 0, 18), t("kli"), 15, A.bitwise_and)
-            ts(t("ki", 18, 36), t("kli"), 4, A.arith_shift_right)
-            ts(t("ki", 0, 18), t("ki", 0, 18), 18, A.mult)
-        quant(t(hq, C1, C1 + 128), t(hs, C1, C1 + 128), t(H, 4 * (E - 128), 4 * E))
-        m = send(dst, "hb%d" % r, t(lq, C1, E), t(hq, C1 + 128 - C2, C1 + 128), [t(hq, C1, C1 + 128)], True)
-        m += send(dst, "hb%d" % r, t(ls, C1, E), t(hs, C1 + 128 - C2, C1 + 128), [t(hs, C1, C1 + 128)])
-        arrives("ha%d" % r, n, [t(lq, 0, C1), t(ls, 0, C1)])
-        arrives("hb%d" % r, m, [t(lq, C1, E), t(ls, C1, E)])
-        if r == 0:
-            tt(t("ki", 36, 54), t("ki", 0, 18), t("ki", 18, 36), A.add)
-            cp(t("ks"), t("ki", 36, 54))
-            ts(t(kk), t(kf), -144.0, A.add, off=t("ks"))
+            actg(t(kk), t(kf), t("ks"), 1.0, -144.0)
+        actg(t(nf), t(kk), t("tt18"), 1.0, 144.0)
+        for b, (c, o) in enumerate(later):
+            if r == 0:
+                unit(b)
+            elif b == 0:
+                pair(0, E, C)
+            ts(c, o, 0.03125, A.mult)
+        quant(t(hq, C1, C1 + 128), t(hs, C1, C1 + 128), t(H, 4 * C1, 4 * C1 + 512))
+        n += send(dst, "ha%d" % r, t(lq, C1, E), t(hq, C1, E), [t(hq, C1, E)], True)
+        n += send(dst, "ha%d" % r, t(ls), t(hs, 0, E), [t(hs, 0, E)])
+        arrives("ha%d" % r, n, [t(lq), t(ls)])
         layer(2, E, C, 12)
         gop(f("n16w"), t(kk), t("tt18"), f("M16n"), A.add)
-        actg(t(nf), t(kk), t("tt18"), 1.0, 144.0)
+        if r == 0:
+            ts(t("oD", 0, 11), t("oC", 1, 22, 2), 0.5, A.mult)
+        if r < 2:
+            cp(t("oK", 0, 3, 2), t(nf, 1, 3))
         scan(f("n16s"), f("d16b"), f("n16w"), A.min, A.max)
+        if r < 2:
+            gop(f("klw"), t(nf), t("oD", 0, 11), f("M144"), A.add)
         ts(t("kt%d" % (r + 1)), f("n16s", 15, 288, 16), 144.0, A.add)
         if r < 2:
             for e in range(4):
                 ts(t("k4t%d" % (r + 1), 20 * e, 20 * e + 18), f("n16s", 15, 288, 16), 4.0, A.mult, 576.0 + e, A.add)
+            scan(f("kls"), f("d16b", 0, 176), f("klw"), A.min, A.max)
             nd = "nd%d" % (r + 1)
             dma("y", "dn%d" % (r + 1), T[nd][:, :], T[nf][0:128:16, :], [t(nf)], [t(nd)])
             lr = "lr%d" % (r + 1)
@@ -490,30 +553,57 @@ def rank_program(g, core, T, topo):
         else:
             dma("y", "dout", T.kp[:, :], T[nf][0:128:16, :], [t(nf)], [])
         if r == 0:
-            quant(t("eq"), t("es"), t("et"))
+            unit(2)
+            unit(3)
+        if r == 2:
             quant(t("vq"), t("vs"), t("vb"))
-        for c0, c1, new, at in ((0, C1, 0, 16), (E - 128, E, 128 - C2, 20)):
-            for b in range(4):
-                mm(bank(at + b, c1 - c0), t("eq", 128 * b, 128 * b + 128), t("es", 128 * b, 128 * b + 128), t(lq, c0, c1), t(ls, c0, c1))
-                k = bank(at + b, c1 - c0)
-                k = (k[0], k[1] + new, k[2], 1)
-                act(t(B, C * b + c0 + new, C * b + c1), k)
+        for b in range(4):
+            mm(bank(b, E), t("eq", 128 * b, 128 * b + 128), t("es", 128 * b, 128 * b + 128), t(lq), t(ls))
+            if b:
+                act(t(B, C * b, C * b + E), bank(b, E))
+            else:
+                cp(t(B, 0, E), bank(0, E))
+                if r < 2:
+                    ts(t("oK", 1, 22, 2), f("kls", 15, 176, 16), 144.0, A.add)
         Xn = "X%d" % (r + 1)
-        for e, a, b in ((0, 0, C), (1, 0, C), (2, 0, C), (3, 0, HS[0][1]), (3, HS[1][0], C)):
-            gop(t(Xn, 4 * a + e, 4 * b, 4), t(B, C * e, C * e + C), t("kt%d" % (r + 1), a // 16, b // 16), t(X, 4 * a + e, 4 * b, 4), A.add)
-        for h in range(2):
-            state(r + 1, h)
-            if r < 2:
-                scores(r + 1, h)
-            if r == 2:
-                q, s = "xq3", "xs3"
-                a, b = HS[h]
-                mm(bank(2 + h, b - a), t("vq"), t("vs"), t(q, a, b), t(s, a, b))
-                dma("y", "dout", T.oc[:, 4 * a:4 * b], T[q][:, a:b].bitcast(dt.uint8), [t(q, a, b)], [])
-                for i in range(4):
-                    dma("y", "dout", T.osc[4 * i:4 * i + 4, a:b], T[s][32 * i:32 * i + 4, a:b], [t(s, a, b)], [])
-                act(t("ysb", a, b), bank(2 + h, b - a))
+
+        def update(e, a, b):
+            if (e, a) in far:
+                tt(t(Xn, 4 * a + e, 4 * b, 4), t(BG, C * (e - 2) + a, C * (e - 2) + b), t(X, 4 * a + e, 4 * b, 4), A.add)
+            else:
+                gop(t(Xn, 4 * a + e, 4 * b, 4), t(B, C * e, C * e + C), t("kt%d" % (r + 1), a // 16, b // 16), t(X, 4 * a + e, 4 * b, 4), A.add)
+
+        (a0, b0), (a1, b1) = HS
+        far = ((3, a0), (3, a1), (2, a1))
+        for e, a in far:
+            b = b0 if a == a0 else b1
+            actg(t(BG, C * (e - 2) + a, C * (e - 2) + b), t(B, C * e, C * e + C), t("kt%d" % (r + 1), a // 16, b // 16))
+        if r < 2:
+            for e, a, b in ((0, 0, C), (1, 0, C), (2, a0, b0), (3, a0, b0), (3, a1, b1)):
+                update(e, a, b)
+            state(r + 1, 0)
+            scores(r + 1, 0)
+            update(2, a1, b1)
+            above(16, 23, 142, r)
+            state(r + 1, 1)
+            scores(r + 1, 1)
+        else:
+            for h, (a, b) in enumerate(HS):
+                for e in range(4):
+                    if (h, e) != (1, 0):
+                        update(e, a, b)
+                if h == 0:
+                    update(0, *HS[1])
+                state(3, h)
+                mm(bank(4 + h, b - a), t("vq"), t("vs"), t("xq3", a, b), t("xs3", a, b))
+                dma("y", "dout", T.oc[:, 4 * a:4 * b], T.xq3[:, a:b].bitcast(dt.uint8), [t("xq3", a, b)], [])
+                if h:
+                    cp(t("ysb", a, b), bank(4 + h, b - a))
+                else:
+                    act(t("ysb", a, b), bank(4 + h, b - a))
                 dma("s", "dout", T.y[:, a:b], T.ysb[:, a:b], [t("ysb", a, b)], [])
+            for i in range(4):
+                dma("y", "dout", T.osc[4 * i:4 * i + 4, :], T.xs3[32 * i:32 * i + 4, :], [t("xs3")], [])
     need("y", "dout", total["dout"])
     need("q", "sent", total["sent"])
     for sem in ("v", "s", "p", "q"):

from concourse.bass import DstId, RemoteDMATransfer
from concourse.mybir import dt, AluOpType, AxisListType, ActivationFunctionType

C, HALF, E = 288, 144, 224
MASKS = [4, 1, 2]
HS = ((0, 160), (160, 288))
C1 = 128
C2 = E - C1
F4 = "float8_e4m3fn_x4"
SEG = 18

SCRATCH = {
    "ub": ("sbuf", [128, 512], "bfloat16"), "vb": ("sbuf", [128, 512], "bfloat16"), "et": ("sbuf", [128, 516], "bfloat16"),
    "one": ("sbuf", [128, 516], "bfloat16"),
    "uq": ("sbuf", [128, 128], F4), "us": ("sbuf", [128, 128], "uint8"),
    "ur": ("sbuf", [128, 128], F4), "urs": ("sbuf", [128, 128], "uint8"),
    "vq": ("sbuf", [128, 128], F4), "vs": ("sbuf", [128, 128], "uint8"),
    "eq": ("sbuf", [128, 512], F4), "es": ("sbuf", [128, 512], "uint8"),
    "wq": ("sbuf", [128, 512], F4), "wp": ("sbuf", [128, 512], "uint8"),
    "kli": ("sbuf", [128, 18], "int32"), "ki": ("sbuf", [128, 54], "int32"),
    "klf": ("sbuf", [128, 18], "float32"), "kld": ("dram", [128, 18], "float32"), "lk0": ("dram", [128, 18], "float32"),
    "nd1": ("dram", [128, 18], "float32"), "nd2": ("dram", [128, 18], "float32"),
    "lk1": ("dram", [128, 18], "float32"), "lk2": ("dram", [128, 18], "float32"),
    "kf0": ("sbuf", [128, C], "float32"), "kf1": ("sbuf", [128, C], "float32"), "kf2": ("sbuf", [128, C], "float32"),
    "pI": ("sbuf", [128, 8], "int32"), "uI": ("sbuf", [128, 24], "int32"), "pF": ("sbuf", [128, 24], "float32"),
    "cI": ("sbuf", [128, 48], "int32"),
    "uo": ("sbuf", [128, 24], "uint16"), "ks": ("sbuf", [128, 18], "uint16"),
    "oC": ("sbuf", [128, 28], "uint16"), "oI": ("sbuf", [128, 28], "uint16"),
    "oD": ("sbuf", [128, 12], "uint16"), "oK": ("sbuf", [128, 24], "uint16"), "oA": ("sbuf", [128, 6], "uint16"), "oE": ("sbuf", [128, 4], "uint16"),
    "oT0": ("sbuf", [128, 10], "uint16"), "oT1": ("sbuf", [128, 6], "uint16"), "oT2": ("sbuf", [128, 6], "uint16"), "oT3": ("sbuf", [128, 6], "uint16"),
    "tt18": ("sbuf", [128, 18], "uint16"),
    "ps": ("psum", [128, 4096], "float32"),
    "ysb": ("sbuf", [128, C], "float32"),
}
for _i in range(4):
    SCRATCH["X%d" % _i] = ("sbuf", [128, 4 * C], "bfloat16")
    SCRATCH["xq%d" % _i] = ("sbuf", [128, C], F4)
    SCRATCH["xs%d" % _i] = ("sbuf", [128, C], "uint8")
    SCRATCH["kt%d" % _i] = ("sbuf", [128, 18], "uint16")
for _i in range(3):
    SCRATCH["XK%d" % _i] = ("sbuf", [128, 4 * C], "bfloat16")
    SCRATCH["XC%d" % _i] = ("sbuf", [128, 4 * C], "bfloat16")
    SCRATCH["ZG%d" % _i] = ("sbuf", [128, 2 * C], "bfloat16")
    SCRATCH["BG%d" % _i] = ("sbuf", [128, 2 * C], "bfloat16")
    SCRATCH["Z%d" % _i] = ("sbuf", [128, 4 * C], "bfloat16")
    SCRATCH["H%d" % _i] = ("sbuf", [128, 4 * (C1 + 128)], "bfloat16")
    SCRATCH["B%d" % _i] = ("sbuf", [128, 4 * C], "bfloat16")
    SCRATCH["zq%d" % _i] = ("sbuf", [128, C1 + 256], F4)
    SCRATCH["zs%d" % _i] = ("sbuf", [128, C1 + 256], "uint8")
    SCRATCH["hq%d" % _i] = ("sbuf", [128, C1 + 128], F4)
    SCRATCH["hs%d" % _i] = ("sbuf", [128, C1 + 128], "uint8")
    SCRATCH["lq%d" % _i] = ("sbuf", [128, E], F4)
    SCRATCH["ls%d" % _i] = ("sbuf", [128, E], "uint8")
    SCRATCH["k4t%d" % _i] = ("sbuf", [128, 80], "uint16")
    SCRATCH["nf%d" % _i] = ("sbuf", [128, C], "float32")
    SCRATCH["kk%d" % _i] = ("sbuf", [128, C], "float32")
_ROWS = {
    "t16": 288, "t32": 32, "M16n": 288, "tmp": 288, "pos": 16, "bb": 16, "bo": 16, "a1": 16, "a2": 16, "mem": 32, "rk": 32,
    "cb": 16, "cu": 16, "su": 16, "en": 16, "hi": 16, "t8": 80, "e8": 80, "JA": 72, "JB": 144, "M144": 176,
}
_ROWS2 = {
    "sg": 288, "fx": 144, "sw": 32, "val": 448, "K": 448, "lk": 176, "uk": 176, "lz": 192, "ls": 192, "ue": 176, "ek": 64, "ez": 64, "es": 64,
    "BT": 320, "M": 288, "MS": 288, "M8": 144,
    "sf": 288, "wv": 288, "Fa": 160, "Fb": 160, "Fc": 160, "Fd": 160, "RD": 128, "La": 160, "Lb": 160, "Lc": 160, "Ld": 160,
    "ts": 160, "rs": 128, "fc": 288, "fj": 144, "J": 80, "x": 288, "z": 288, "xs": 288,
    "n16w": 288, "n16s": 288, "d16b": 288, "klw": 176, "kls": 176,
}
_ROW_OF = {"F1": "Fa", "F2": "Fb", "F3": "Fc", "F4": "Fd", "F5": "Fa", "F9": "Fb", "F13": "Fc", "F22": "Fd",
           "L4": "La", "L6": "Lb", "L10": "Lc", "C10": "La", "L19": "Lb", "L28": "Ld", "C28": "La", "L50": "Lb", "L72": "Lc"}
OFF = {}
for _b, _t, _d in (("F", _ROWS, "float32"), ("G", _ROWS2, "bfloat16")):
    _n = 0
    for _k, _v in _t.items():
        OFF[_k] = (_b, _n, _v)
        _n += (_v + 15) // 16 * 16
    SCRATCH[_b] = ("sbuf", [128, _n], _d)

SEMAPHORES = ["v", "s", "p", "q", "sent", "dx0", "dx1", "dk", "du", "dw", "dv", "dkl", "dn1", "dn2", "df0", "df1", "df2", "dout",
              "lr0", "lr1", "lr2", "ha0", "ha1", "ha2", "hb0", "hb1", "hb2", "dc0", "dc1", "dc2", "dd0", "dd1", "dd2"]


def rank_program(g, core, T, topo):
    rank = T.rank_of(core)
    if rank is None:
        return
    A = AluOpType
    COPY, IDENT, SIGN = ActivationFunctionType.Copy, ActivationFunctionType.Identity, ActivationFunctionType.Sign
    queue = {"v": g.vector, "s": g.scalar, "p": g.tensor, "q": g, "y": g.sync}
    total, known, log = {}, {}, {}

    def f(name, a=0, b=None, step=1):
        o = OFF[_ROW_OF.get(name, name)]
        return (o[0], o[1] + a, o[1] + (o[2] if b is None else b), step)

    def t(name, a=0, b=None, step=1):
        return (name, a, SCRATCH[name][1][1] if b is None else b, step)

    def ap(x):
        return T[x[0]][:, x[1]:x[2]:x[3]] if x[3] != 1 else T[x[0]][:, x[1]:x[2]]

    def ind(win, off):
        return ap(win).indirect(ap(off))

    def clash(x, y):
        if x[0] != y[0] or x[1] >= y[2] or y[1] >= x[2]:
            return False
        if x[3] > 1 and y[3] > 1 and (x[3] % y[3] == 0 or y[3] % x[3] == 0) and (x[1] - y[1]) % min(x[3], y[3]):
            return False
        return True

    def need(q, sem, val):
        if known.get((q, sem), 0) < val:
            queue[q].wait_ge(T.sem[sem], val)
            known[(q, sem)] = val

    def order(q, reads, writes):
        want = {}
        for rw, views in ((0, reads), (1, writes)):
            for x in views:
                for y, w, sem, val in log.get(x[0], ()):
                    if (rw or w) and clash(x, y):
                        want[sem] = max(want.get(sem, 0), val if val else total[sem])
        for sem in want:
            need(q, sem, want[sem])

    def note(sem, val, reads, writes):
        for x in writes:
            log[x[0]] = [e for e in log.get(x[0], []) if not (e[0][1] >= x[1] and e[0][2] <= x[2] and (x[3] == 1 or x == e[0]))]
            log[x[0]].append((x, 1, sem, val))
        for x in reads:
            log.setdefault(x[0], []).append((x, 0, sem, val))

    def run(q, call, reads, writes):
        psum = [("ps", x[1] // 512 * 512, x[1] // 512 * 512 + 512, 1) for x in reads + writes if x[0] == "ps"]
        reads, writes = [x for x in reads if x[0] != "ps"], [x for x in writes if x[0] != "ps"] + psum
        order(q, reads, writes)
        total[q] = total.get(q, 0) + 1
        call().then_inc(T.sem[q], 1)
        note(q, total[q], reads, writes)

    def dma(q, sem, out, in_, reads, writes):
        order(q, reads, writes)
        total[sem] = total.get(sem, 0) + 16
        queue[q].dma_start(out, in_).then_inc(T.sem[sem], 16)
        note(sem, 0, reads, writes)

    def tt(out, a, b, op):
        run("v", lambda: g.vector.tensor_tensor(ap(out), ap(a), ap(b), op), [a, b], [out])

    def ts(out, a, s1, op0, s2=None, op1=None, off=None):
        sc = [x for x in (s1, s2, off) if isinstance(x, tuple)]
        u1 = ap(s1) if isinstance(s1, tuple) else s1
        u2 = ap(s2) if isinstance(s2, tuple) else s2
        src = ap(a) if off is None else ind(a, off)
        if op1 is None:
            run("v", lambda: g.vector.tensor_scalar(ap(out), src, u1, None, op0), [a] + sc, [out])
        else:
            run("v", lambda: g.vector.tensor_scalar(ap(out), src, u1, u2, op0, op1), [a] + sc, [out])

    def cp(out, a):
        run("v", lambda: g.vector.tensor_copy(ap(out), ap(a)), [a], [out])

    def gat(out, win, off):
        run("v", lambda: g.vector.tensor_copy(ap(out), ind(win, off)), [win, off], [out])

    def gop(out, win, off, b, op):
        run("v", lambda: g.vector.tensor_tensor(ap(out), ind(win, off), ap(b), op), [win, off, b], [out])

    def scan(out, d0, d1, op0, op1, first=0.0):
        run("v", lambda: g.vector.tensor_tensor_scan(ap(out), ap(d0), ap(d1), first, op0, op1), [d0, d1], [out])

    def act(out, a, scale=1.0):
        run("s", lambda: g.scalar.activation(ap(out), ap(a), COPY, scale=scale), [a], [out])

    def actf(out, a, func, scale, bias):
        if isinstance(bias, tuple):
            run("s", lambda: g.scalar.activation(ap(out), ap(a), func, bias=ap(bias), scale=scale), [a, bias], [out])
        else:
            run("s", lambda: g.scalar.activation(ap(out), ap(a), func, bias=bias, scale=scale), [a], [out])

    def equal(out, a, col, tmp):
        actf(tmp, a, ActivationFunctionType.Abs, -1.0, col)
        actf(out, tmp, ActivationFunctionType.Relu, -1.0, 1.0)

    def actg(out, win, off, scale=1.0, bias=None):
        if bias is None:
            run("s", lambda: g.scalar.activation(ap(out), ind(win, off), COPY, scale=scale), [win, off], [out])
        else:
            run("s", lambda: g.scalar.activation(ap(out), ind(win, off), IDENT, bias=bias), [win, off], [out])

    def fill(out, c):
        run("v", lambda: g.vector.memset(ap(out), c), [], [out])

    def quant(q, s, a):
        run("v", lambda: g.vector.quantize_mx(ap(q), ap(s), ap(a)), [a], [q, s])

    def mm(out, l, ls, r, rs):
        run("p", lambda: g.tensor.matmul_mx(ap(out), ap(l), ap(ls), ap(r), ap(rs), True, True), [l, ls, r, rs], [out])

    def iota(out, pattern, base=0, cm=0):
        if out[0] in "FG":
            run("q", lambda: g.iota(ap(out), pattern, base, cm, allow_small_or_imprecise_dtypes=True), [], [out])
        else:
            run("q", lambda: g.iota(ap(out), pattern, base, cm), [], [out])

    def bank(i, n):
        i %= 8
        return ("ps", 512 * i, 512 * i + n, 1)

    def send(dst, sem, out, in_, reads, bits=False):
        order("q", reads, [])
        rid, pid = topo.addr(dst, core)
        n = len(topo.engines(core, dst))
        o, i = (ap(out).bitcast(dt.uint8), ap(in_).bitcast(dt.uint8)) if bits else (ap(out), ap(in_))
        if SCRATCH[out[0]][0] == "dram":
            o, i = T[out[0]][:, :], T[in_[0]][:, :]
        total["sent"] = total.get("sent", 0) + n
        g.remote_dma(o, i, T.sem[sem], T.sem.sent, pid, rid, topo.mask(core, dst))
        return n

    def arrives(sem, n, writes):
        total[sem] = total.get(sem, 0) + n
        note(sem, 0, [], writes)

    dma("y", "dx0", T.X0[:, 0:640], T.x[:, 0:640], [], [t("X0", 0, 640)])
    dma("s", "dk", T.kli[:, :], T.kl[:, :], [], [t("kli")])
    dma("s", "du", T.ub[:, :], T.u[:, :], [], [t("ub")])
    dma("y", "dx1", T.X0[:, 640:1152], T.x[:, 640:1152], [], [t("X0", 640, 1152)])

    iota(t("pI", 0, 1), [[0, 1]], 0, 1)
    iota(t("uI", 0, 10), [[16, 10]])
    iota(f("t32"), [[1, 32]])
    iota(f("bb", 0, 9), [[-1, 9]], 8)
    iota(f("bo", 0, 10), [[0, 5], [16, 2]])
    iota(f("wv", 128, 288, 2), [[-64, 5], [-2, 16]], 286)
    iota(f("sw", 0, 32, 16), [[-2, 2]], 1)
    iota(f("wv", 0, 144, 2), [[4, 72]])
    iota(f("t16"), [[0, 18], [1, 16]])
    iota(f("fx"), [[0, 144]], -1)
    iota(f("lz"), [[0, 6], [512, 32]])
    iota(f("lz", 32, 33), [[0, 1]], 512)
    iota(f("ls", 176, 192), [[0, 16]])
    iota(f("t8"), [[0, 10], [1, 8]])
    iota(f("ez"), [[0, 4], [512, 16]])
    iota(f("J"), [[2, 80]])
    iota(f("x", 3, 288, 4), [[0, 72]])
    iota(f("z", 3, 288, 4), [[0, 72]], 1)
    partner = [T.cores[rank ^ m] for m in MASKS]

    def pcol(i):
        return t("pF", i, i + 1)

    fill(("G", OFF["sf"][1] + 1, OFF["ts"][1], 2), 0.0)
    ts(t("pI", 1, 2), t("pI", 0, 1), 15, A.bitwise_and)
    ts(t("pI", 2, 3), t("pI", 0, 1), 16, A.bitwise_and)
    ts(t("pI", 3, 4), t("pI", 0, 1), 14, A.bitwise_and)
    ts(t("pI", 4, 5), t("pI", 0, 1), 1, A.bitwise_and)
    for a, b, c in ((0, 1, 2.0), (1, 2, 4.0), (2, 4, 8.0), (4, 8, 16.0), (8, 16, 32.0), (16, 32, 64.0)):
        fill(f("rk", a, b), c)
    cp(t("pF", 1, 5), t("pI", 1, 5))
    P16, ODD16, P14, PAR = [pcol(i) for i in range(1, 5)]
    for a, b, step, c in ((0, 12, 1, 2), (2, 3, 1, 4), (12, 24, 1, 284), (14, 15, 1, 282)):
        fill(t("oC", a, b, step), c)
    cp(t("uo", 0, 10), t("uI", 0, 10))
    ts(f("mem", 0, 16), f("t32", 0, 16), P16, A.is_equal)
    ts(f("pos", 0, 10), t("uI", 0, 10), P16, A.add)
    actf(pcol(5), P16, IDENT, -1.0 / 64, 31.0 / 64)
    actf(pcol(6), ODD16, IDENT, 11.0, 0.0)
    actf(pcol(9), P14, IDENT, 0.5, 0.0)
    actf(pcol(14), PAR, IDENT, -2.0, 1.0)
    actf(f("cb", 0, 9), f("pos", 0, 9), IDENT, 2.0, -147.5)
    actf(f("cu", 0, 9), f("pos", 0, 9), IDENT, 4.0, -143.0)
    actf(pcol(15), pcol(14), IDENT, -4.0, 0.5)
    fill(t("oI"), 0)
    tt(f("a1"), f("mem", 0, 16), f("rk", 0, 16), A.mult)
    ts(f("a2", 0, 9), f("bb", 0, 9), f("mem", 0, 1), A.add, -1.0, A.add)
    fill(t("oI", 4, 7, 2), 16)
    run("v", lambda: g.vector.tensor_reduce(ap(pcol(7)), ap(f("a1")), AxisListType.X, A.add), [f("a1")], [pcol(7)])
    fill(t("oI", 16, 19, 2), 16)
    ts(t("ki", 2, 32), f("rk", 2, 32), pcol(5), A.mult, -0.49, A.add)
    ts(f("a2", 0, 9), f("a2", 0, 9), pcol(7), A.mult, 0.25, A.mult)
    for a, b, step, c in ((1, 10, 2, 0), (13, 22, 2, 0), (24, 28, 1, 5)):
        ts(t("oI", a, b, step), f("bo", c, c + len(range(a, b, step))), f("mem", 0, 1), A.mult, P16, A.add)
    ts(f("a2", 0, 9), f("a2", 0, 9), P16, A.add, -0.25, A.add)
    tt(f("mem", 2, 32), t("ki", 2, 32), f("t32", 2, 32), A.is_equal)
    cp(t("cI", 0, 9), f("a2", 0, 9))
    ts(t("k4t0", 0, 18), t("kli"), 4, A.mult, 0, A.add)
    tt(f("sw", 1, 16), f("mem", 2, 32, 2), f("mem", 3, 32, 2), A.subtract)
    ts(t("oC", 1, 10, 2), t("cI", 0, 5), 2.0, A.mult)
    ts(t("oC", 13, 22, 2), t("cI", 0, 5), -2.0, A.mult, 286.0, A.add)
    ts(t("oC", 24, 28), t("cI", 5, 9), -2.0, A.mult, 286.0, A.add)
    for e in range(1, 4):
        ts(t("k4t0", 20 * e, 20 * e + 18), t("kli"), 4, A.mult, e, A.add)
    cp(t("kt0"), t("kli"))
    cp(t("klf"), t("kli"))
    dma("y", "dkl", T.kld[:, :], T.klf[:, :], [t("klf")], [t("kld")])
    need("y", "dx1", 16)
    dma("y", "dw", T.wq[:, 0:512].bitcast(dt.uint8), T.wc[:, :], [], [t("wq")])
    dma("y", "dw", T.wp[:, 0:512], T.ws[:, :], [], [t("wp")])
    for a, step, c in ((0, 4, 1), (1, 4, -1), (2, 4, -1), (0, 32, 0)):
        iota(f("z", a, 288, step), [[0, 288 // step]], c)
    arrives("lr0", send(partner[0], "lr0", t("lk0"), t("kld"), [t("kld")]), [t("lk0")])
    iota(f("JB"), [[256, 9], [17, 16]])
    iota(f("JA"), [[256, 9], [33, 8]])
    iota(f("d16b"), [[0, 18], [16384, 16]], -8192)
    equal(f("M16n", 0, 160), f("t16", 0, 160), P16, f("tmp", 0, 160))

    def weights(a, b, q):
        if q == "s":
            actg(f("val", 16 * a, 16 * b), f("wv"), t("oC", a, b))
        else:
            gop(f("K", 16 * a, 16 * b), f("sw", 0, 17), t("oI", a, b), f("val", 16 * a, 16 * b), A.mult)

    weights(0, 11, "s")
    quant(t("uq"), t("us"), t("ub"))
    run("v", lambda: g.vector.tensor_copy(T.ur[:, 0:128].bitcast(dt.uint32), T.uq[:, 0:128].bitcast(dt.uint32).indirect(T.uo[:, 0:8])),
        [t("uq"), t("uo")], [t("ur")])
    run("s", lambda: g.scalar.activation(T.urs[:, 0:128], T.us[:, 0:128].indirect(T.uo[:, 0:8]), COPY), [t("us"), t("uo")], [t("urs")])
    weights(12, 23, "s")
    weights(0, 11, "v")
    act(f("M", 0, 288, 2), f("M16n", 0, 144), 256.0)
    act(f("M", 1, 288, 2), f("M16n", 1, 145), -4096.0)
    weights(24, 28, "s")

    def picks():
        equal(f("e8"), f("t8"), pcol(9), f("tmp", 0, 80))
        act(f("MS"), f("M"), 1.0 / 64)
        act(f("M8", 0, 144, 2), f("e8", 0, 72), 4.0)
        act(f("M8", 1, 144, 2), f("e8", 1, 73), -64.0)

    def state(r, h):
        a, b = HS[h]
        quant(t("xq%d" % r, a, b), t("xs%d" % r, a, b), t("X%d" % r, 4 * a, 4 * b))

    def scores(r, h):
        a, b = HS[h]
        mm(bank(2 + h, b - a), t("ur"), t("urs"), t("xq%d" % r, a, b), t("xs%d" % r, a, b))

    state(0, 0)
    state(0, 1)
    scores(0, 0)
    scores(0, 1)
    fill(f("fx", 143, 144), 0.5)
    weights(12, 23, "v")
    run("q", lambda: g.iota(T.one[:, 0:516], [[0, 516]], 1, 0, allow_small_or_imprecise_dtypes=True), [], [t("one")])
    run("q", lambda: g.affine_select(T.et[:, 0:516], T.one[:, 0:516], [[-1, 516]], A.is_equal, 0.0, 3, 4), [t("one")], [t("et")])

    def unit(b):
        quant(t("eq", 128 * b, 128 * b + 128), t("es", 128 * b, 128 * b + 128), t("et", 3 - b, 515 - b))

    def marks():
        actf(pcol(10), P16, IDENT, -1.0 / 16, pcol(14))
        actf(pcol(11), pcol(9), IDENT, -1.0 / 16, 0.0)
        actf(pcol(12), f("M16n", 0, 1), IDENT, -0.5, 0.0)
        actf(pcol(10), pcol(10), IDENT, 1.0, PAR)
        actf(f("JA"), f("JA"), IDENT, 1.0 / 16, pcol(11))
        actf(pcol(10), pcol(10), IDENT, 1.0, -1.0)
        actf(f("JA", 0, 1), f("JA", 0, 1), IDENT, 1.0, pcol(12))
        actf(f("JB"), f("JB"), IDENT, 1.0 / 16, pcol(10))
        actf(f("M16n", 160, 288), f("M16n", 0, 128), IDENT, 4096.0, -4096.0)
        actf(f("M16n", 0, 160), f("M16n", 0, 160), IDENT, 4096.0, -4096.0)
        actf(f("M144"), f("M16n", 0, 176), IDENT, 1.0, -144.0)
        actf(f("JB", 0, 1), f("JB", 0, 1), IDENT, 1.0, pcol(12))

    def above(a, b, c, r):
        ts(t("oK", a, b, 2), f("pos", 0, (b - a + 1) // 2), 0.0, A.mult, t("nf%d" % r, c, c + 1), A.add)

    def even(n):
        return f(n, 0, 160, 2)

    def table(i, row):
        scan(f("ts"), f(row), f("M", 0, 160), A.max, A.add, -4096.0)
        return lambda: ts(t("oT%d" % i, 0, 5), f("ts", 30, 160, 32), -256.0, A.add)

    def lowest(out, win, i, other):
        gop(even(out), f(win), t("oT%d" % i, 0, 5), other if isinstance(other, tuple) else even(other), A.min)

    for r in range(3):
        X, XK, XC, Z, H, B, kt = ["%s%d" % (n, r) for n in ("X", "XK", "XC", "Z", "H", "B", "kt")]
        zq, zs, hq, hs, lq, ls, nf, kk = ["%s%d" % (n, r) for n in ("zq", "zs", "hq", "hs", "lq", "ls", "nf", "kk")]
        kf, lk, ZG, BG = "kf%d" % r, "lk%d" % r, "ZG%d" % r, "BG%d" % r

        def xk(e):
            actg(t(XK, C * e, C * e + C), t(X), t("k4t%d" % r, 20 * e, 20 * e + 18), 0.5)
            if e % 2:
                a, b = C * (e - 1), C * (e + 1)
                dma("y", "d%s%d" % ("cd"[e // 2], r), T[XC][:, a:b], T[XK][:, a:b], [t(XK, a, b)], [t(XC, a, b)])

        xk(0)
        xk(1)
        for h in range(2):
            ts(f("sg", HS[h][0], HS[h][1]), bank(2 + h, HS[h][1] - HS[h][0]), 0.0, A.is_gt, -0.5, A.add)
            if r and h == 0:
                for a, b, c in ((4, 11, 1), (12, 13, 142), (14, 15, 141)):
                    above(a, b, c, r - 1)
        if r:
            xk(2)
        else:
            picks()
        def bits():
            gop(f("sf", 0, 288, 2), f("sg"), t(kt, 0, 9), f("fx"), A.max)

        if r == 0:
            bits()
        win, off = ("sg", "oK") if r else ("sf", "oC")
        gop(f("lk"), f(win), t(off, 0, 11), f("K", 0, 176), A.mult)
        gop(f("uk"), f(win), t(off, 12, 23), f("K", 192, 368), A.mult)
        scan(f("ls", 0, 176), f("lz", 16, 192), f("lk"), A.min, A.max)
        scan(f("ue"), f("lz", 16, 192), f("uk"), A.min, A.max)
        xk(3 if r else 2)
        for a, b in ((0, 32), (160, 16)):
            run("v", lambda: g.vector.transpose(ap(f("BT", a, a + 160)), ap(f("ls", b, b + 160))), [f("ls", b, b + 160)], [f("BT", a, a + 160)])
        ts(t("oA", 0, 5), f("ue", 32, 176, 32), pcol(6), A.add)
        gat(even("F1"), f("BT"), t("oA", 0, 5))
        end = table(0, "F1")
        tt(even("L4"), even("F1"), f("J"), A.min)
        end()
        if r == 0:
            xk(3)
            weights(24, 28, "v")
        for i in range(16):
            dma("y", "df%d" % r, T[kf][i:128:16, :], T[lk][:, :], [t(lk)], [(kf, i, C, 16)])
        if r == 1:
            dma("y", "dv", T.vb[:, :], T.v[:, :], [], [t("vb")])
        for a, b in (("F2", "F1"), ("F3", "F2"), ("F4", "F3"), ("F5", "F4")):
            if r == 0 and a == "F2":
                gat(even(a), f(b), t("oT0", 0, 5))
            else:
                actg(even(a), f(b), t("oT0", 0, 5))
        if r:
            bits()
        tt(even("L4"), even("L4"), even("F2"), A.min)
        gop(f("ek"), f("sf"), t("oC", 24, 28), f("K", 384, 448), A.mult)
        scan(f("fc"), f("sf"), f("MS"), A.max, A.add, -64.0)
        scan(f("es"), f("ez"), f("ek"), A.min, A.max)
        tt(even("L4"), even("L4"), even("F3"), A.min)
        ts(t("oE"), f("es", 15, 64, 16), pcol(6), A.add)
        end = table(1, "F4")
        tt(even("L6"), even("L4"), even("F4"), A.min)
        end()
        scan(f("fj"), f("sf", 0, 144), f("M8"), A.max, A.add, -64.0)
        tt(even("L6"), even("L6"), even("F5"), A.min)
        actg(even("F9"), f("F5"), t("oT1", 0, 5))
        actg(even("F13"), f("F9"), t("oT1", 0, 5))
        tt(f("x", 31, 288, 32), f("fc", 30, 288, 32), f("cb", 0, 9), A.add)
        lowest("L10", "L6", 1, "L4")
        end = table(2, "F9")
        cp(even("C10"), even("L10"))
        end()
        if r:
            ts(f("su", 0, 9), f("fc", 30, 288, 32), -4.0, A.add, 2.0, A.mult)
        actg(even("F22"), f("F13"), t("oT2", 0, 5))
        actg(f("RD", 0, 128, 2), f("BT"), t("oE"))
        if r == 0:
            ts(t("ki", 0, 18), t("kli"), 15, A.bitwise_and)
            ts(t("ki", 18, 36), t("kli"), 4, A.arith_shift_right)
            ts(t("ki", 0, 18), t("ki", 0, 18), 18, A.mult)
        lowest("L19", "L10", 2, "C10")
        if r == 0:
            ts(f("su", 0, 9), f("fc", 30, 288, 32), -4.0, A.add, 2.0, A.mult)
        ts(f("en", 0, 9), f("fj", 14, 144, 16), pcol(14), A.mult, pcol(15), A.add)
        end = table(3, "F22")
        lowest("L28", "L19", 2, "L10")
        end()
        cp(even("C28"), even("L28"))
        actf(t(H, 4 * E, 4 * C1 + 512), f("t16", 0, 4 * (C1 + 128 - E)), IDENT, 0.0, 0.0)
        if r == 0:
            marks()
        else:
            actg(t(kk), t(kf), t(kt), 1.0, -144.0)
        scan(f("rs"), f("RD"), f("M", 0, 128), A.max, A.add, -4096.0)
        lowest("L50", "L28", 3, "C28")
        ts(t("oT0", 5, 9), f("rs", 30, 128, 32), -256.0, A.add)
        lowest("L72", "L50", 3, "L28")
        tt(f("z", 31, 288, 32), f("su", 0, 9), f("en", 0, 9), A.mult)
        gop(f("x", 0, 288, 2), f("L72"), t("oT0", 0, 9), f("JB"), A.is_equal)
        tt(f("x", 1, 288, 4), f("L72", 0, 144, 2), f("JA", 0, 72), A.is_equal)
        if r == 0:
            tt(t("ki", 36, 54), t("ki", 0, 18), t("ki", 18, 36), A.add)
        scan(f("xs"), f("z"), f("x"), A.mult, A.add)
        if r == 0:
            cp(t("ks"), t("ki", 36, 54))
        ts(t("tt18", 0, 9), f("xs", 31, 288, 32), 144.0, A.add)
        tt(f("hi", 0, 9), f("cu", 0, 9), f("xs", 31, 288, 32), A.subtract)

        def pair(e, a, b):
            if e >= 2:
                tt(t(Z, 4 * a + e, 4 * b, 4), t(ZG, C * (e - 2) + a, C * (e - 2) + b), t(XC, C * e + a, C * e + b), A.add)
            else:
                gop(t(Z, 4 * a + e, 4 * b, 4), t(XK, C * e, C * e + C), t("tt18", a // 16, b // 16), t(XC, C * e + a, C * e + b), A.add)

        def layer(i, a, b, at):
            for e in range(4):
                if (i, e) != (2, 0) or r == 0:
                    pair(e, a, b)
                if i == 0 and e == 0:
                    cp(t("tt18", 9, 18), f("hi", 0, 9))
                    for a2, b2 in ((0, C1), (C1, E)):
                        for e2 in (2, 3):
                            actg(t(ZG, C * (e2 - 2) + a2, C * (e2 - 2) + b2), t(XK, C * e2, C * e2 + C), t("tt18", a2 // 16, b2 // 16))
            n = max(128, b - a)
            p = 0 if i == 0 else C1 + 128 * (i - 1)
            q, s = t(zq, p, p + n), t(zs, p, p + n)
            quant(q, s, t(Z, 4 * (b - n), 4 * b))
            for k in range(4):
                mm(bank(at + k, n), t("wq", 128 * k, 128 * k + 128), t("wp", 128 * k, 128 * k + 128), q, s)
                o, c = bank(at + k, n), t(B, C * k + a, C * k + b) if i == 2 else t(H, 4 * a + k, 4 * b, 4)
                o = (o[0], o[2] - (b - a), o[2], 1)
                if i == 1 and k % 2:
                    later.append((c, o))
                else:
                    act(c, o, 0.03125)

        later = []
        layer(0, 0, C1, 4)
        layer(1, C1, E, 8)
        quant(t(hq, 0, C1), t(hs, 0, C1), t(H, 0, 4 * C1))
        dst = partner[r]
        n = send(dst, "ha%d" % r, t(lq, 0, C1), t(hq, 0, C1), [t(hq, 0, C1)], True)
        for e in (2, 3):
            actg(t(ZG, C * (e - 2) + E, C * (e - 2) + C), t(XK, C * e, C * e + C), t("tt18", E // 16, C // 16))
        if r == 0:
            actg(t(kk), t(kf), t("ks"), 1.0, -144.0)
        actg(t(nf), t(kk), t("tt18"), 1.0, 144.0)
        for b, (c, o) in enumerate(later):
            if r == 0:
                unit(b)
            elif b == 0:
                pair(0, E, C)
            ts(c, o, 0.03125, A.mult)
        quant(t(hq, C1, C1 + 128), t(hs, C1, C1 + 128), t(H, 4 * C1, 4 * C1 + 512))
        n += send(dst, "ha%d" % r, t(lq, C1, E), t(hq, C1, E), [t(hq, C1, E)], True)
        n += send(dst, "ha%d" % r, t(ls), t(hs, 0, E), [t(hs, 0, E)])
        arrives("ha%d" % r, n, [t(lq), t(ls)])
        layer(2, E, C, 12)
        gop(f("n16w"), t(kk), t("tt18"), f("M16n"), A.add)
        if r == 0:
            ts(t("oD", 0, 11), t("oC", 1, 22, 2), 0.5, A.mult)
        if r < 2:
            cp(t("oK", 0, 3, 2), t(nf, 1, 3))
        scan(f("n16s"), f("d16b"), f("n16w"), A.min, A.max)
        if r < 2:
            gop(f("klw"), t(nf), t("oD", 0, 11), f("M144"), A.add)
        ts(t("kt%d" % (r + 1)), f("n16s", 15, 288, 16), 144.0, A.add)
        if r < 2:
            for e in range(4):
                ts(t("k4t%d" % (r + 1), 20 * e, 20 * e + 18), f("n16s", 15, 288, 16), 4.0, A.mult, 576.0 + e, A.add)
            scan(f("kls"), f("d16b", 0, 176), f("klw"), A.min, A.max)
            nd = "nd%d" % (r + 1)
            dma("y", "dn%d" % (r + 1), T[nd][:, :], T[nf][0:128:16, :], [t(nf)], [t(nd)])
            lr = "lr%d" % (r + 1)
            arrives(lr, send(partner[r + 1], lr, t("lk%d" % (r + 1)), t(nd), [t(nd)]), [t("lk%d" % (r + 1))])
        else:
            dma("y", "dout", T.kp[:, :], T[nf][0:128:16, :], [t(nf)], [])
        if r == 0:
            unit(2)
            unit(3)
        if r == 2:
            quant(t("vq"), t("vs"), t("vb"))
        for b in range(4):
            mm(bank(b, E), t("eq", 128 * b, 128 * b + 128), t("es", 128 * b, 128 * b + 128), t(lq), t(ls))
            if b:
                act(t(B, C * b, C * b + E), bank(b, E))
            else:
                cp(t(B, 0, E), bank(0, E))
                if r < 2:
                    ts(t("oK", 1, 22, 2), f("kls", 15, 176, 16), 144.0, A.add)
        Xn = "X%d" % (r + 1)

        def update(e, a, b):
            if (e, a) in far:
                tt(t(Xn, 4 * a + e, 4 * b, 4), t(BG, C * (e - 2) + a, C * (e - 2) + b), t(X, 4 * a + e, 4 * b, 4), A.add)
            else:
                gop(t(Xn, 4 * a + e, 4 * b, 4), t(B, C * e, C * e + C), t("kt%d" % (r + 1), a // 16, b // 16), t(X, 4 * a + e, 4 * b, 4), A.add)

        (a0, b0), (a1, b1) = HS
        far = ((3, a0), (3, a1), (2, a1))
        for e, a in far:
            b = b0 if a == a0 else b1
            actg(t(BG, C * (e - 2) + a, C * (e - 2) + b), t(B, C * e, C * e + C), t("kt%d" % (r + 1), a // 16, b // 16))
        if r < 2:
            for e, a, b in ((0, 0, C), (1, 0, C), (2, a0, b0), (3, a0, b0), (3, a1, b1)):
                update(e, a, b)
            state(r + 1, 0)
            scores(r + 1, 0)
            update(2, a1, b1)
            above(16, 23, 142, r)
            state(r + 1, 1)
            scores(r + 1, 1)
        else:
            for h, (a, b) in enumerate(HS):
                for e in range(4):
                    if (h, e) != (1, 0):
                        update(e, a, b)
                if h == 0:
                    update(0, *HS[1])
                state(3, h)
                mm(bank(4 + h, b - a), t("vq"), t("vs"), t("xq3", a, b), t("xs3", a, b))
                dma("y", "dout", T.oc[:, 4 * a:4 * b], T.xq3[:, a:b].bitcast(dt.uint8), [t("xq3", a, b)], [])
                if h:
                    cp(t("ysb", a, b), bank(4 + h, b - a))
                else:
                    act(t("ysb", a, b), bank(4 + h, b - a))
                dma("s", "dout", T.y[:, a:b], T.ysb[:, a:b], [t("ysb", a, b)], [])
            for i in range(4):
                dma("y", "dout", T.osc[4 * i:4 * i + 4, :], T.xs3[32 * i:32 * i + 4, :], [t("xs3")], [])
    need("y", "dout", total["dout"])
    need("q", "sent", total["sent"])
    for sem in ("v", "s", "p", "q"):
        need("y", sem, total[sem])
